import numpy as np
import ml_dtypes


def mxq(x, axis, fmt="e4m3"):
    dtype, down = {"e4m3": (ml_dtypes.float8_e4m3fn, 7), "e5m2": (ml_dtypes.float8_e5m2, 14)}[fmt]
    v = np.moveaxis(np.asarray(x, np.float32).astype(ml_dtypes.bfloat16).astype(np.float64), axis, -1)
    blocks = v.reshape(v.shape[:-1] + (-1, 32))
    amax = np.abs(blocks).max(-1, keepdims=True)
    byte = np.maximum(np.where(amax > 0, np.frexp(amax)[1] - 1 + 127, 0) - down, 1)
    scale = np.exp2(byte - 127.0)
    codes = (blocks / scale).astype(np.float32).astype(dtype).astype(np.float64)
    return np.moveaxis((codes * scale).reshape(v.shape), -1, axis)


WIDE = False


def mx_kscale(k):
    if not WIDE:
        return np.ones(k)
    levels = np.array([10, -10, 5, -5, 0])
    if k % 512:
        return np.exp2(np.random.permutation(np.resize(levels, k // 32))).repeat(32)
    a = np.empty((k // 512, 16))
    for p in range(k // 512):
        a[p, :8] = np.random.permutation(np.resize(levels, 8))
        for g in range(8):
            far = levels[np.abs(levels - a[p, g]) >= 10]
            a[p, g + 8] = far[np.random.randint(len(far))]
    return np.exp2(a.ravel()).repeat(32)


BF16 = ml_dtypes.bfloat16


def bf(x):
    return np.asarray(x, np.float32).astype(BF16)


def f64(x):
    return np.asarray(x).astype(np.float64)


M, N, R = 1024, 1536, 512


def positive_part(t):
    return np.maximum(t, 0.0)


def negative_part(t):
    return np.maximum(-t, 0.0)


def draw0():
    s, t = mx_kscale(M), mx_kscale(R)
    return {"x": bf(np.random.standard_normal((M, N)) * 3.0 * s[:, None]),
            "f": bf(np.random.standard_normal((M, R)) * 1.5 / np.sqrt(M) * s[:, None]),
            "g": bf(np.random.uniform(0.1, 1.0, (N, R))),
            "m": bf(np.random.uniform(0.5, 1.5, M) / (s * s)),
            "c": bf(np.random.standard_normal(R) * t),
            "d": bf(np.random.uniform(0.25, 1.25, R) / (t * t))}


def core(x, f, g, m, c, d):
    x, f, g, m, c, d = f64(x), f64(f), f64(g), f64(m), f64(c), f64(d)
    fm = f * m[:, None]
    fmq = mxq(fm, 0, "e4m3")
    p = mxq(x, 0, "e4m3").T @ fmq
    a = mxq(f, 0, "e4m3").T @ fmq
    gcq = mxq(g * c[None, :], 1, "e4m3")
    e = c * d
    an = negative_part(a) * e[:, None]
    ap = positive_part(a) * e[:, None]
    gn = gcq @ mxq(an, 0, "e4m3")
    gp = gcq @ mxq(ap, 0, "e4m3")
    num = positive_part(p) + gn
    den = negative_part(p) + gp
    return g * np.sqrt(num / den)


def e4m3fn_bytes(y):
    return np.clip(np.asarray(y, np.float64), -448.0, 448.0).astype(np.float32).astype(ml_dtypes.float8_e4m3fn).view(np.uint8)


def e4m3fn_values(b):
    return np.asarray(b, np.uint8).view(ml_dtypes.float8_e4m3fn).astype(np.float64)


def setup_inputs():
    d = draw0()
    x0 = np.asarray(d['x']).astype(np.float64)
    s = (np.max(np.abs(x0), axis=(1,), keepdims=True) / 448.0).astype(np.float32)
    out = {}
    for k, v in d.items():
        if k == 'x':
            out['x_bytes'] = e4m3fn_bytes(x0 / s.astype(np.float64))
            out['x_scale'] = s
        else:
            out[k] = v
    return out


def reference(x_bytes, x_scale, f, g, m, c, d):
    return core(e4m3fn_values(x_bytes) * x_scale.astype(np.float64), f, g, m, c, d)

@@ -1,0 +1,365 @@
+from contextlib import ExitStack
+
+import concourse.mybir as mybir
+from concourse.masks import make_identity
+
+M, N, R = 1024, 1536, 512
+
+F32 = mybir.dt.float32
+BF16 = mybir.dt.bfloat16
+U32 = mybir.dt.uint32
+U8 = mybir.dt.uint8
+FP8 = mybir.dt.float8_e4m3fn
+FP8X4 = mybir.dt.float8_e4m3fn_x4
+ALU = mybir.AluOpType
+ACT = mybir.ActivationFunctionType
+
+P = 128
+G = 2
+T = 4
+W = 512
+NC = N // W
+NT = N // P
+
+FLOPS = 2 * N * R * M + 2 * R * R * M + 2 * 2 * N * R * R
+
+
+def tile_seminmfsquarerootupdate_kernel(tc, x_bytes, x_scale, f, g, m, c, d, out):
+    nc = tc.nc
+    with ExitStack() as ctx:
+        const = ctx.enter_context(tc.tile_pool(name="const", bufs=1))
+        work = ctx.enter_context(tc.tile_pool(name="work", bufs=2))
+        psum = ctx.enter_context(tc.psum_pool(name="psum", bufs=2))
+
+        ident = const.tile([P, P], F32, name="ident")
+        warm = const.tile([P, 1], F32, name="warm")
+        warm2 = const.tile([P, 1], F32, name="warm2")
+        m_sb = const.tile([P, G, T], BF16, name="m_sb")
+        xs_sb = const.tile([P, G, T], F32, name="xs_sb")
+        c_row = const.tile([P, R], BF16, name="c_row")
+        c_col = const.tile([P, T], BF16, name="c_col")
+        d_col = const.tile([P, T], BF16, name="d_col")
+        e_neg = const.tile([P, T], F32, name="e_neg")
+
+        f_raw = []
+        f_int = []
+        fm_int = []
+        f_q = []
+        f_s = []
+        fm_q = []
+        fm_s = []
+        xb = []
+        for k in range(G):
+            f_raw.append(const.tile([P, T, R], BF16, name="f_raw%d" % k, align_bytes=64))
+            f_int.append(const.tile([P, T, P, T], BF16, name="f_int%d" % k, align_bytes=64))
+            fm_int.append(const.tile([P, R, T], BF16, name="fm_int%d" % k, align_bytes=64))
+            f_q.append(const.tile([P, R], U32, name="f_q%d" % k, align_bytes=64))
+            f_s.append(const.tile([P, R], U8, name="f_s%d" % k, align_bytes=64))
+            fm_q.append(const.tile([P, R], U32, name="fm_q%d" % k, align_bytes=64))
+            fm_s.append(const.tile([P, R], U8, name="fm_s%d" % k, align_bytes=64))
+            halves = []
+            for h in range(2):
+                halves.append(const.tile([P, 2, N], U8, name="xb%d%d" % (k, h), align_bytes=64))
+            xb.append(halves)
+        x_q = {}
+        x_s = {}
+        for ch in range(NC):
+            for k in range(G):
+                x_q[ch, k] = const.tile([P, W], U32, name="x_q%d%d" % (ch, k), align_bytes=64)
+                x_s[ch, k] = const.tile([P, W], U8, name="x_s%d%d" % (ch, k), align_bytes=64)
+        g_sb = []
+        g_q = []
+        g_s = []
+        for ch in range(NC):
+            g_sb.append(const.tile([P, 4, R], BF16, name="g_sb%d" % ch, align_bytes=64))
+            g_q.append(const.tile([P, W], U32, name="g_q%d" % ch, align_bytes=64))
+            g_s.append(const.tile([P, W], U8, name="g_s%d" % ch, align_bytes=64))
+        an_int = const.tile([P, R, T], BF16, name="an_int", align_bytes=64)
+        ap_int = const.tile([P, R, T], BF16, name="ap_int", align_bytes=64)
+        an_q = const.tile([P, R], U32, name="an_q", align_bytes=64)
+        an_s = const.tile([P, R], U8, name="an_s", align_bytes=64)
+        ap_q = const.tile([P, R], U32, name="ap_q", align_bytes=64)
+        ap_s = const.tile([P, R], U8, name="ap_s", align_bytes=64)
+
+        f_v = f.rearrange("(k p t) r -> k p t r", p=P, t=T)
+        x_v = x_bytes.rearrange("(k p t) n -> k p t n", p=P, t=T)
+        g_v = g.rearrange("(h i p) r -> h p i r", i=4, p=P)
+
+        with tc.manual_schedule():
+            nc.scalar.dma_start(out=m_sb[:], in_=m.rearrange("(k p t) -> p k t", p=P, t=T))
+            nc.scalar.dma_start(out=xs_sb[:], in_=x_scale.rearrange("(k p t) o -> p k (t o)", p=P, t=T))
+            nc.gpsimd.dma_start(out=c_col[:], in_=c.rearrange("(p t) -> p t", t=T))
+            nc.gpsimd.dma_start(out=d_col[:], in_=d.rearrange("(p t) -> p t", t=T))
+            nc.gpsimd.dma_start(out=c_row[:], in_=c.partition_broadcast(P))
+            for k in range(G):
+                nc.sync.dma_start(out=f_raw[k][:], in_=f_v[k])
+            for h in range(2):
+                nc.sync.dma_start(out=xb[0][h][:], in_=x_v[0, :, 2 * h : 2 * h + 2, :])
+            nc.sync.dma_start(out=g_sb[0][:], in_=g_v[0])
+            for h in range(2):
+                nc.sync.dma_start(out=xb[1][h][:], in_=x_v[1, :, 2 * h : 2 * h + 2, :])
+            for ch in range(1, NC):
+                nc.sync.dma_start(out=g_sb[ch][:], in_=g_v[ch])
+            nc.vector.memset(warm[:], 1.0)
+            nc.scalar.activation(out=warm2[:], in_=warm[:], func=ACT.Abs_reciprocal_sqrt)
+            make_identity(nc, ident[:])
+
+            def interleave_f(eng_copy, k, lo, hi):
+                eng_copy(
+                    out=f_int[k][:, lo:hi, :, :],
+                    in_=f_raw[k][:].rearrange("p j (q t) -> p t q j", t=T)[:, lo:hi, :, :],
+                )
+
+            def make_fm(k):
+                nc.vector.tensor_tensor(
+                    out=fm_int[k][:].rearrange("p (q t) j -> p q t j", t=T),
+                    in0=f_int[k][:].rearrange("p t q j -> p q t j"),
+                    in1=m_sb[:, k, :].unsqueeze(1).unsqueeze(1).to_broadcast([P, P, T, T]),
+                    op=ALU.mult,
+                )
+
+            def quant(codes, scales, src):
+                nc.vector.quantize_mx(out=codes.bitcast(FP8X4), scales=scales, in_=src)
+
+            def quant_f(k):
+                quant(f_q[k][:], f_s[k][:], f_int[k][:].rearrange("p t q j -> p (t q j)"))
+
+            def quant_fm(k):
+                quant(fm_q[k][:], fm_s[k][:], fm_int[k][:].rearrange("p r j -> p (r j)"))
+
+            xw = {}
+            xi = {}
+
+            def widen(ch, k, t):
+                if t == 0:
+                    xw[ch, k] = work.tile([P, T, W], BF16, name="xw", align_bytes=64, bufs=4)
+                nc.scalar.activation(
+                    out=xw[ch, k][:, t, :],
+                    in_=xb[k][t // 2][:, t % 2, ch * W : (ch + 1) * W].bitcast(FP8),
+                    func=ACT.Copy,
+                    scale=xs_sb[:, k, t : t + 1],
+                )
+
+            def interleave_x(eng_copy, ch, k):
+                xi[ch, k] = work.tile([P, W, T], BF16, name="xi", align_bytes=64, bufs=3)
+                eng_copy(
+                    out=xi[ch, k][:].rearrange("p (c i) t -> p c t i", i=4),
+                    in_=xw[ch, k][:].rearrange("p t (c i) -> p c t i", i=4),
+                )
+
+            def quant_x(ch, k):
+                quant(x_q[ch, k][:], x_s[ch, k][:], xi[ch, k][:].rearrange("p c t -> p (c t)"))
+
+            gc = {}
+            gi = {}
+
+            def gain(ch):
+                gc[ch] = work.tile([P, 4, R], BF16, name="gc", align_bytes=64, bufs=2)
+                nc.vector.tensor_tensor(
+                    out=gc[ch][:],
+                    in0=g_sb[ch][:],
+                    in1=c_row[:].unsqueeze(1).to_broadcast([P, 4, R]),
+                    op=ALU.mult,
+                )
+
+            def transpose_g(ch, b):
+                tr = psum.tile([P, 2, 2, P], F32, name="tr", tag="tr", bufs=2)
+                for i in range(2):
+                    words = gc[ch][:, 2 * b + i, :].bitcast(F32)
+                    for u in range(2):
+                        nc.tensor.transpose(tr[:, i, u, :], words[:, u : R // 2 : 2], ident[:])
+                return tr
+
+            def empty_g(ch, b, tr):
+                if b == 0:
+                    gi[ch] = work.tile([P, W, T], BF16, name="gi", align_bytes=64, bufs=2)
+                words = gi[ch][:].rearrange("p r t -> p (r t)").bitcast(F32)
+                nc.scalar.copy(
+                    out=words[:, b * W : (b + 1) * W].rearrange("p (i r u) -> p i r u", i=2, u=2),
+                    in_=tr[:].rearrange("p i u r -> p i r u"),
+                )
+
+            def quant_g(ch):
+                quant(g_q[ch][:], g_s[ch][:], gi[ch][:].rearrange("p r t -> p (r t)"))
+
+            def a_chunk(n, tag):
+                ps = psum.tile([P, T, P], F32, name="a_ps%d" % n, tag=tag, bufs=2)
+                for t in range(T):
+                    for k in range(G):
+                        nc.tensor.matmul_mx(
+                            out=ps[:, t, :],
+                            lhsT=f_q[k][:, t * P : (t + 1) * P].bitcast(FP8X4),
+                            lhsT_scale=f_s[k][:, t * P : (t + 1) * P],
+                            rhs=fm_q[k][:, n * P : (n + 1) * P].bitcast(FP8X4),
+                            rhs_scale=fm_s[k][:, n * P : (n + 1) * P],
+                            start=(k == 0),
+                            stop=(k == G - 1),
+                        )
+                return ps
+
+            def a_parts(n, ps, dst, op):
+                nc.vector.scalar_tensor_tensor(
+                    out=dst[:, n * P : (n + 1) * P, :],
+                    in0=ps[:].rearrange("p t n -> p n t"),
+                    scalar=0.0,
+                    in1=e_neg[:].unsqueeze(1).to_broadcast([P, P, T]),
+                    op0=op,
+                    op1=ALU.mult,
+                )
+
+            pp = {}
+            gg = {}
+            dd = {}
+            rp = {}
+
+            def mm_p(ps, i, k, start, stop):
+                ch, o = divmod(i * P, W)
+                nc.tensor.matmul_mx(
+                    out=ps[:],
+                    lhsT=x_q[ch, k][:, o : o + P].bitcast(FP8X4),
+                    lhsT_scale=x_s[ch, k][:, o : o + P],
+                    rhs=fm_q[k][:].bitcast(FP8X4),
+                    rhs_scale=fm_s[k][:],
+                    start=start,
+                    stop=stop,
+                )
+
+            def mm_g(ps, i, q, s, start, stop):
+                ch, o = divmod(i * P, W)
+                nc.tensor.matmul_mx(
+                    out=ps[:],
+                    lhsT=g_q[ch][:, o : o + P].bitcast(FP8X4),
+                    lhsT_scale=g_s[ch][:, o : o + P],
+                    rhs=q[:].bitcast(FP8X4),
+                    rhs_scale=s[:],
+                    start=start,
+                    stop=stop,
+                )
+
+            def matmuls(i):
+                pp[i] = psum.tile([P, R], F32, name="pp", tag="pp", bufs=2)
+                mm_p(pp[i], i, 0, True, False)
+                mm_p(pp[i], i, 1, False, True)
+                gg[i] = psum.tile([P, R], F32, name="gg", tag="gg", bufs=2)
+                mm_g(gg[i], i, an_q, an_s, True, True)
+                dd[i] = psum.tile([P, R], F32, name="dd", tag="dd", bufs=2)
+                mm_p(dd[i], i, 0, True, False)
+                mm_p(dd[i], i, 1, False, False)
+                mm_g(dd[i], i, ap_q, ap_s, False, True)
+
+            def relu(i):
+                rp[i] = work.tile([P, R], F32, name="rp", bufs=4)
+                nc.scalar.activation(out=rp[i][:], in_=pp[i][:], func=ACT.Relu)
+
+            nd = {}
+            rs = {}
+
+            def num_den(i):
+                nd[i] = work.tile([P, 2, R], F32, name="nd", bufs=4)
+                nc.vector.scalar_tensor_tensor(
+                    out=nd[i][:, 0, :], in0=gg[i][:], scalar=1e-30, in1=rp[i][:], op0=ALU.max, op1=ALU.add
+                )
+                nc.vector.tensor_tensor(out=nd[i][:, 1, :], in0=rp[i][:], in1=dd[i][:], op=ALU.subtract)
+
+            def rsqrt(i):
+                rs[i] = work.tile([P, 2, R], F32, name="rs", bufs=4)
+                nc.scalar.activation(out=rs[i][:], in_=nd[i][:], func=ACT.Abs_reciprocal_sqrt)
+
+            def times_g(i):
+                nc.gpsimd.tensor_tensor(
+                    out=nd[i][:, 0, :], in0=nd[i][:, 0, :], in1=g_sb[i // 4][:, i % 4, :], op=ALU.mult
+                )
+
+            def finish(i):
+                nc.vector.tensor_tensor(out=rs[i][:, 0, :], in0=rs[i][:, 0, :], in1=rs[i][:, 1, :], op=ALU.mult)
+
+            def finish2(i):
+                res = work.tile([P, R], F32, name="res", bufs=3)
+                nc.vector.tensor_tensor(out=res[:], in0=rs[i][:, 0, :], in1=nd[i][:, 0, :], op=ALU.mult)
+                nc.sync.dma_start(out=out[i * P : (i + 1) * P, :], in_=res[:])
+
+            interleave_f(nc.vector.tensor_copy, 0, 0, 2)
+            interleave_f(nc.vector.tensor_copy, 0, 2, 4)
+            interleave_f(nc.scalar.copy, 1, 0, 4)
+            nc.vector.scalar_tensor_tensor(out=e_neg[:], in0=c_col[:], scalar=-1.0, in1=d_col[:], op0=ALU.mult, op1=ALU.mult)
+            make_fm(0)
+            quant_f(0)
+            quant_fm(0)
+            make_fm(1)
+            quant_f(1)
+            quant_fm(1)
+            gain(0)
+            for k in range(G):
+                for t in range(T):
+                    widen(0, k, t)
+            a_ps = []
+            for n in range(4):
+                a_ps.append(a_chunk(n, ["pp", "gg", "dd", "pp"][n]))
+            tr00 = transpose_g(0, 0)
+            tr01 = transpose_g(0, 1)
+            interleave_x(nc.scalar.copy, 0, 1)
+            empty_g(0, 0, tr00)
+            empty_g(0, 1, tr01)
+            for n in range(4):
+                a_parts(n, a_ps[n], an_int, ALU.min)
+                a_parts(n, a_ps[n], ap_int, ALU.max)
+            for t in range(T):
+                widen(1, 0, t)
+            interleave_x(nc.vector.tensor_copy, 0, 0)
+            quant(an_q[:], an_s[:], an_int[:].rearrange("p r t -> p (r t)"))
+            quant(ap_q[:], ap_s[:], ap_int[:].rearrange("p r t -> p (r t)"))
+            quant_x(0, 0)
+            quant_g(0)
+            quant_x(0, 1)
+            matmuls(0)
+            relu(0)
+            gain(1)
+            for t in range(T):
+                widen(1, 1, t)
+            tr10 = transpose_g(1, 0)
+            tr11 = transpose_g(1, 1)
+            empty_g(1, 0, tr10)
+            empty_g(1, 1, tr11)
+            interleave_x(nc.vector.tensor_copy, 1, 0)
+
+            s_fill = {
+                0: [lambda: interleave_x(nc.scalar.copy, 1, 1)],
+                1: [lambda: widen(2, 0, 0)],
+                2: [lambda: widen(2, 0, 1), lambda: widen(2, 0, 2)],
+                3: [lambda: widen(2, 0, 3), lambda: widen(2, 1, 0)],
+                4: [lambda: widen(2, 1, 1), lambda: widen(2, 1, 2), lambda: widen(2, 1, 3)],
+                5: [lambda: interleave_x(nc.scalar.copy, 2, 1)],
+            }
+            v_fill = {
+                0: [lambda: quant_x(1, 0)],
+                1: [lambda: quant_g(1)],
+                2: [lambda: gain(2), lambda: quant_x(1, 1)],
+                5: [lambda: interleave_x(nc.vector.tensor_copy, 2, 0), lambda: quant_g(2)],
+                6: [lambda: quant_x(2, 0), lambda: quant_x(2, 1)],
+            }
+            tr2 = []
+            for i in range(NT):
+                if i + 1 < NT:
+                    matmuls(i + 1)
+                    relu(i + 1)
+                num_den(i)
+                for fill in s_fill.get(i, []):
+                    fill()
+                if i == 3:
+                    tr2.append(transpose_g(2, 0))
+                    tr2.append(transpose_g(2, 1))
+                if i == 4:
+                    empty_g(2, 0, tr2[0])
+                    empty_g(2, 1, tr2[1])
+                rsqrt(i)
+                if i >= 2:
+                    finish(i - 2)
+                for fill in v_fill.get(i, []):
+                    fill()
+                if i >= 2:
+                    finish2(i - 2)
+                times_g(i)
+            finish(NT - 2)
+            finish2(NT - 2)
+            finish(NT - 1)
+            finish2(NT - 1)

@@ -17,9 +17,8 @@ ACT = mybir.ActivationFunctionType
 P = 128
 G = 2
 T = 4
-W = 512
-NC = N // W
 NT = N // P
+CHUNKS = ((0, 512), (512, 1024))
 
 FLOPS = 2 * N * R * M + 2 * R * R * M + 2 * 2 * N * R * R
 
@@ -40,46 +39,41 @@ def tile_seminmfsquarerootupdate_kernel(tc, x_bytes, x_scale, f, g, m, c, d, out
         c_col = const.tile([P, T], BF16, name="c_col")
         d_col = const.tile([P, T], BF16, name="d_col")
         e_neg = const.tile([P, T], F32, name="e_neg")
+        e_pos = const.tile([P, T], F32, name="e_pos")
 
-        f_raw = []
-        f_int = []
-        fm_int = []
-        f_q = []
-        f_s = []
-        fm_q = []
-        fm_s = []
-        xb = []
+        f_raw = [const.tile([P, T, R], BF16, name="f_raw%d" % k, align_bytes=64) for k in range(G)]
+        f_int = const.tile([P, G, T, P, T], BF16, name="f_int", align_bytes=64)
+        fm_int = const.tile([P, G, R, T], BF16, name="fm_int", align_bytes=64)
+        f_q = const.tile([P, G, R], U32, name="f_q", align_bytes=64)
+        f_s = const.tile([P, G, R], U8, name="f_s", align_bytes=64)
+        fm_q = const.tile([P, G, R], U32, name="fm_q", align_bytes=64)
+        fm_s = const.tile([P, G, R], U8, name="fm_s", align_bytes=64)
+        xb = {}
         for k in range(G):
-            f_raw.append(const.tile([P, T, R], BF16, name="f_raw%d" % k, align_bytes=64))
-            f_int.append(const.tile([P, T, P, T], BF16, name="f_int%d" % k, align_bytes=64))
-            fm_int.append(const.tile([P, R, T], BF16, name="fm_int%d" % k, align_bytes=64))
-            f_q.append(const.tile([P, R], U32, name="f_q%d" % k, align_bytes=64))
-            f_s.append(const.tile([P, R], U8, name="f_s%d" % k, align_bytes=64))
-            fm_q.append(const.tile([P, R], U32, name="fm_q%d" % k, align_bytes=64))
-            fm_s.append(const.tile([P, R], U8, name="fm_s%d" % k, align_bytes=64))
-            halves = []
             for h in range(2):
-                halves.append(const.tile([P, 2, N], U8, name="xb%d%d" % (k, h), align_bytes=64))
-            xb.append(halves)
+                xb[k, h] = const.tile([P, 2, N], U8, name="xb%d%d" % (k, h), align_bytes=64)
         x_q = {}
         x_s = {}
-        for ch in range(NC):
-            for k in range(G):
-                x_q[ch, k] = const.tile([P, W], U32, name="x_q%d%d" % (ch, k), align_bytes=64)
-                x_s[ch, k] = const.tile([P, W], U8, name="x_s%d%d" % (ch, k), align_bytes=64)
-        g_sb = []
+        x_w = {}
+        x_i = {}
         g_q = []
         g_s = []
-        for ch in range(NC):
-            g_sb.append(const.tile([P, 4, R], BF16, name="g_sb%d" % ch, align_bytes=64))
-            g_q.append(const.tile([P, W], U32, name="g_q%d" % ch, align_bytes=64))
-            g_s.append(const.tile([P, W], U8, name="g_s%d" % ch, align_bytes=64))
-        an_int = const.tile([P, R, T], BF16, name="an_int", align_bytes=64)
-        ap_int = const.tile([P, R, T], BF16, name="ap_int", align_bytes=64)
-        an_q = const.tile([P, R], U32, name="an_q", align_bytes=64)
-        an_s = const.tile([P, R], U8, name="an_s", align_bytes=64)
-        ap_q = const.tile([P, R], U32, name="ap_q", align_bytes=64)
-        ap_s = const.tile([P, R], U8, name="ap_s", align_bytes=64)
+        g_i = []
+        for ch, (lo, w) in enumerate(CHUNKS):
+            for k in range(G):
+                x_w[ch, k] = const.tile([P, T, w], BF16, name="x_w%d%d" % (ch, k), align_bytes=64)
+                x_i[ch, k] = const.tile([P, w, T], BF16, name="x_i%d%d" % (ch, k), align_bytes=64)
+                x_q[ch, k] = const.tile([P, w], U32, name="x_q%d%d" % (ch, k), align_bytes=64)
+                x_s[ch, k] = const.tile([P, w], U8, name="x_s%d%d" % (ch, k), align_bytes=64)
+            g_q.append(const.tile([P, w], U32, name="g_q%d" % ch, align_bytes=64))
+            g_s.append(const.tile([P, w], U8, name="g_s%d" % ch, align_bytes=64))
+            g_i.append(const.tile([P, w, T], BF16, name="g_i%d" % ch, align_bytes=64))
+        g_sb = [const.tile([P, 4, R], BF16, name="g_sb%d" % h, align_bytes=64) for h in range(3)]
+        a_int = const.tile([P, 2, R, T], BF16, name="a_int", align_bytes=64)
+        a_q = const.tile([P, 2, R], U32, name="a_q", align_bytes=64)
+        a_s = const.tile([P, 2, R], U8, name="a_s", align_bytes=64)
+        num = const.tile([P, NT, R], F32, name="num")
+        den = const.tile([P, NT, R], F32, name="den")
 
         f_v = f.rearrange("(k p t) r -> k p t r", p=P, t=T)
         x_v = x_bytes.rearrange("(k p t) n -> k p t n", p=P, t=T)
@@ -88,32 +82,39 @@ def tile_seminmfsquarerootupdate_kernel(tc, x_bytes, x_scale, f, g, m, c, d, out
         with tc.manual_schedule():
             nc.scalar.dma_start(out=m_sb[:], in_=m.rearrange("(k p t) -> p k t", p=P, t=T))
             nc.scalar.dma_start(out=xs_sb[:], in_=x_scale.rearrange("(k p t) o -> p k (t o)", p=P, t=T))
+            nc.gpsimd.dma_start(out=c_row[:], in_=c.partition_broadcast(P))
             nc.gpsimd.dma_start(out=c_col[:], in_=c.rearrange("(p t) -> p t", t=T))
             nc.gpsimd.dma_start(out=d_col[:], in_=d.rearrange("(p t) -> p t", t=T))
-            nc.gpsimd.dma_start(out=c_row[:], in_=c.partition_broadcast(P))
-            for k in range(G):
-                nc.sync.dma_start(out=f_raw[k][:], in_=f_v[k])
             for h in range(2):
-                nc.sync.dma_start(out=xb[0][h][:], in_=x_v[0, :, 2 * h : 2 * h + 2, :])
+                nc.sync.dma_start(out=f_raw[0][:, :, h * 256 : (h + 1) * 256], in_=f_v[0, :, :, h * 256 : (h + 1) * 256])
+            nc.sync.dma_start(out=f_raw[1][:], in_=f_v[1])
+            for h in range(2):
+                nc.sync.dma_start(out=xb[0, h][:], in_=x_v[0, :, 2 * h : 2 * h + 2, :])
             nc.sync.dma_start(out=g_sb[0][:], in_=g_v[0])
             for h in range(2):
-                nc.sync.dma_start(out=xb[1][h][:], in_=x_v[1, :, 2 * h : 2 * h + 2, :])
-            for ch in range(1, NC):
-                nc.sync.dma_start(out=g_sb[ch][:], in_=g_v[ch])
+                nc.sync.dma_start(out=xb[1, h][:], in_=x_v[1, :, 2 * h : 2 * h + 2, :])
+            for h in range(1, 3):
+                nc.sync.dma_start(out=g_sb[h][:], in_=g_v[h])
             nc.vector.memset(warm[:], 1.0)
             nc.scalar.activation(out=warm2[:], in_=warm[:], func=ACT.Abs_reciprocal_sqrt)
             make_identity(nc, ident[:])
 
-            def interleave_f(eng_copy, k, lo, hi):
-                eng_copy(
-                    out=f_int[k][:, lo:hi, :, :],
-                    in_=f_raw[k][:].rearrange("p j (q t) -> p t q j", t=T)[:, lo:hi, :, :],
-                )
+            copy_on = {"V": nc.vector.tensor_copy, "S": nc.scalar.copy}
+            mul_on = {"V": nc.vector.tensor_tensor, "G": nc.gpsimd.tensor_tensor}
+
+            def copy(e, dst, src):
+                if e == "G":
+                    nc.gpsimd.tensor_scalar(out=dst, in0=src, scalar1=1.0, scalar2=0.0, op0=ALU.mult, op1=ALU.add)
+                else:
+                    copy_on[e](out=dst, in_=src)
+
+            def interleave_f(e, k, lo, hi):
+                copy(e, f_int[:, k, :, lo // 4 : hi // 4, :], f_raw[k][:, :, lo:hi].rearrange("p j (q t) -> p t q j", t=T))
 
             def make_fm(k):
                 nc.vector.tensor_tensor(
-                    out=fm_int[k][:].rearrange("p (q t) j -> p q t j", t=T),
-                    in0=f_int[k][:].rearrange("p t q j -> p q t j"),
+                    out=fm_int[:, k, :, :].rearrange("p (q t) j -> p q t j", t=T),
+                    in0=f_int[:, k, :, :, :].rearrange("p t q j -> p q t j"),
                     in1=m_sb[:, k, :].unsqueeze(1).unsqueeze(1).to_broadcast([P, P, T, T]),
                     op=ALU.mult,
                 )
@@ -121,66 +122,56 @@ def tile_seminmfsquarerootupdate_kernel(tc, x_bytes, x_scale, f, g, m, c, d, out
             def quant(codes, scales, src):
                 nc.vector.quantize_mx(out=codes.bitcast(FP8X4), scales=scales, in_=src)
 
-            def quant_f(k):
-                quant(f_q[k][:], f_s[k][:], f_int[k][:].rearrange("p t q j -> p (t q j)"))
+            def quant_f():
+                quant(f_q[:].rearrange("p k r -> p (k r)"), f_s[:].rearrange("p k r -> p (k r)"), f_int[:].rearrange("p k t q j -> p (k t q j)"))
 
-            def quant_fm(k):
-                quant(fm_q[k][:], fm_s[k][:], fm_int[k][:].rearrange("p r j -> p (r j)"))
+            def quant_fm():
+                quant(fm_q[:].rearrange("p k r -> p (k r)"), fm_s[:].rearrange("p k r -> p (k r)"), fm_int[:].rearrange("p k r j -> p (k r j)"))
 
-            xw = {}
-            xi = {}
+            def widen(e, ch, k, t):
+                lo, w = CHUNKS[ch]
+                src = xb[k, t // 2][:, t % 2, lo : lo + w].bitcast(FP8)
+                if e == "S":
+                    nc.scalar.activation(out=x_w[ch, k][:, t, :], in_=src, func=ACT.Copy, scale=xs_sb[:, k, t : t + 1])
+                else:
+                    nc.vector.tensor_scalar(out=x_w[ch, k][:, t, :], in0=src, scalar1=xs_sb[:, k, t : t + 1], scalar2=None, op0=ALU.mult)
 
-            def widen(ch, k, t):
-                if t == 0:
-                    xw[ch, k] = work.tile([P, T, W], BF16, name="xw", align_bytes=64, bufs=4)
-                nc.scalar.activation(
-                    out=xw[ch, k][:, t, :],
-                    in_=xb[k][t // 2][:, t % 2, ch * W : (ch + 1) * W].bitcast(FP8),
-                    func=ACT.Copy,
-                    scale=xs_sb[:, k, t : t + 1],
-                )
-
-            def interleave_x(eng_copy, ch, k):
-                xi[ch, k] = work.tile([P, W, T], BF16, name="xi", align_bytes=64, bufs=3)
-                eng_copy(
-                    out=xi[ch, k][:].rearrange("p (c i) t -> p c t i", i=4),
-                    in_=xw[ch, k][:].rearrange("p t (c i) -> p c t i", i=4),
-                )
+            def interleave_x(e, ch, k, lo, hi):
+                dst = x_i[ch, k][:, lo:hi, :]
+                src = x_w[ch, k][:, :, lo:hi]
+                if e == "G":
+                    copy(e, dst, src.rearrange("p t c -> p c t"))
+                else:
+                    copy(e, dst.rearrange("p (c i) t -> p c t i", i=4), src.rearrange("p t (c i) -> p c t i", i=4))
 
             def quant_x(ch, k):
-                quant(x_q[ch, k][:], x_s[ch, k][:], xi[ch, k][:].rearrange("p c t -> p (c t)"))
+                quant(x_q[ch, k][:], x_s[ch, k][:], x_i[ch, k][:].rearrange("p c t -> p (c t)"))
 
             gc = {}
-            gi = {}
+            trs = {}
 
-            def gain(ch):
-                gc[ch] = work.tile([P, 4, R], BF16, name="gc", align_bytes=64, bufs=2)
-                nc.vector.tensor_tensor(
-                    out=gc[ch][:],
-                    in0=g_sb[ch][:],
-                    in1=c_row[:].unsqueeze(1).to_broadcast([P, 4, R]),
-                    op=ALU.mult,
-                )
+            def gain(e, h):
+                gc[h] = work.tile([P, 4, R], BF16, name="gc", align_bytes=64, bufs=2)
+                mul_on[e](out=gc[h][:], in0=g_sb[h][:], in1=c_row[:].unsqueeze(1).to_broadcast([P, 4, R]), op=ALU.mult)
 
-            def transpose_g(ch, b):
+            def transpose_g(h, b):
                 tr = psum.tile([P, 2, 2, P], F32, name="tr", tag="tr", bufs=2)
                 for i in range(2):
-                    words = gc[ch][:, 2 * b + i, :].bitcast(F32)
+                    words = gc[h][:, 2 * b + i, :].bitcast(F32)
                     for u in range(2):
                         nc.tensor.transpose(tr[:, i, u, :], words[:, u : R // 2 : 2], ident[:])
-                return tr
+                trs[h, b] = tr
 
-            def empty_g(ch, b, tr):
-                if b == 0:
-                    gi[ch] = work.tile([P, W, T], BF16, name="gi", align_bytes=64, bufs=2)
-                words = gi[ch][:].rearrange("p r t -> p (r t)").bitcast(F32)
-                nc.scalar.copy(
-                    out=words[:, b * W : (b + 1) * W].rearrange("p (i r u) -> p i r u", i=2, u=2),
-                    in_=tr[:].rearrange("p i u r -> p i r u"),
-                )
+            def empty_g(e, h, b):
+                ch = min(h, 1)
+                words = g_i[ch][:].rearrange("p r t -> p (r t)").bitcast(F32)
+                o = (h * 2 + b) * 512 - 2 * CHUNKS[ch][0]
+                copy(e, words[:, o : o + 512].rearrange("p (i r u) -> p i r u", i=2, u=2), trs[h, b][:].rearrange("p i u r -> p i r u"))
 
             def quant_g(ch):
-                quant(g_q[ch][:], g_s[ch][:], gi[ch][:].rearrange("p r t -> p (r t)"))
+                quant(g_q[ch][:], g_s[ch][:], g_i[ch][:].rearrange("p r t -> p (r t)"))
+
+            a_ps = {}
 
             def a_chunk(n, tag):
                 ps = psum.tile([P, T, P], F32, name="a_ps%d" % n, tag=tag, bufs=2)
@@ -188,21 +179,22 @@ def tile_seminmfsquarerootupdate_kernel(tc, x_bytes, x_scale, f, g, m, c, d, out
                     for k in range(G):
                         nc.tensor.matmul_mx(
                             out=ps[:, t, :],
-                            lhsT=f_q[k][:, t * P : (t + 1) * P].bitcast(FP8X4),
-                            lhsT_scale=f_s[k][:, t * P : (t + 1) * P],
-                            rhs=fm_q[k][:, n * P : (n + 1) * P].bitcast(FP8X4),
-                            rhs_scale=fm_s[k][:, n * P : (n + 1) * P],
+                            lhsT=f_q[:, k, t * P : (t + 1) * P].bitcast(FP8X4),
+                            lhsT_scale=f_s[:, k, t * P : (t + 1) * P],
+                            rhs=fm_q[:, k, n * P : (n + 1) * P].bitcast(FP8X4),
+                            rhs_scale=fm_s[:, k, n * P : (n + 1) * P],
                             start=(k == 0),
                             stop=(k == G - 1),
                         )
-                return ps
+                a_ps[n] = ps
 
-            def a_parts(n, ps, dst, op):
+            def a_part(n, z):
+                e, op = ((e_neg, ALU.min), (e_pos, ALU.max))[z]
                 nc.vector.scalar_tensor_tensor(
-                    out=dst[:, n * P : (n + 1) * P, :],
-                    in0=ps[:].rearrange("p t n -> p n t"),
+                    out=a_int[:, z, n * P : (n + 1) * P, :],
+                    in0=a_ps[n][:].rearrange("p t n -> p n t"),
                     scalar=0.0,
-                    in1=e_neg[:].unsqueeze(1).to_broadcast([P, P, T]),
+                    in1=e[:].unsqueeze(1).to_broadcast([P, P, T]),
                     op0=op,
                     op1=ALU.mult,
                 )
@@ -212,154 +204,242 @@ def tile_seminmfsquarerootupdate_kernel(tc, x_bytes, x_scale, f, g, m, c, d, out
             dd = {}
             rp = {}
 
-            def mm_p(ps, i, k, start, stop):
-                ch, o = divmod(i * P, W)
-                nc.tensor.matmul_mx(
-                    out=ps[:],
-                    lhsT=x_q[ch, k][:, o : o + P].bitcast(FP8X4),
-                    lhsT_scale=x_s[ch, k][:, o : o + P],
-                    rhs=fm_q[k][:].bitcast(FP8X4),
-                    rhs_scale=fm_s[k][:],
-                    start=start,
-                    stop=stop,
-                )
+            def chunk_of(i):
+                for ch, (lo, w) in enumerate(CHUNKS):
+                    if lo <= i * P < lo + w:
+                        return ch, i * P - lo
 
-            def mm_g(ps, i, q, s, start, stop):
-                ch, o = divmod(i * P, W)
+            def mm_p(i):
+                pp[i] = psum.tile([P, R], F32, name="pp", tag="pp", bufs=2)
+                ch, o = chunk_of(i)
+                for k in range(G):
+                    nc.tensor.matmul_mx(
+                        out=pp[i][:],
+                        lhsT=x_q[ch, k][:, o : o + P].bitcast(FP8X4),
+                        lhsT_scale=x_s[ch, k][:, o : o + P],
+                        rhs=fm_q[:, k, :].bitcast(FP8X4),
+                        rhs_scale=fm_s[:, k, :],
+                        start=(k == 0),
+                        stop=(k == G - 1),
+                    )
+
+            def mm_g(ps, i, z):
+                ch, o = chunk_of(i)
                 nc.tensor.matmul_mx(
                     out=ps[:],
                     lhsT=g_q[ch][:, o : o + P].bitcast(FP8X4),
                     lhsT_scale=g_s[ch][:, o : o + P],
-                    rhs=q[:].bitcast(FP8X4),
-                    rhs_scale=s[:],
-                    start=start,
-                    stop=stop,
+                    rhs=a_q[:, z, :].bitcast(FP8X4),
+                    rhs_scale=a_s[:, z, :],
+                    start=True,
+                    stop=True,
                 )
 
-            def matmuls(i):
-                pp[i] = psum.tile([P, R], F32, name="pp", tag="pp", bufs=2)
-                mm_p(pp[i], i, 0, True, False)
-                mm_p(pp[i], i, 1, False, True)
+            def mm_n(i):
                 gg[i] = psum.tile([P, R], F32, name="gg", tag="gg", bufs=2)
-                mm_g(gg[i], i, an_q, an_s, True, True)
+                mm_g(gg[i], i, 0)
+
+            def mm_d(i):
                 dd[i] = psum.tile([P, R], F32, name="dd", tag="dd", bufs=2)
-                mm_p(dd[i], i, 0, True, False)
-                mm_p(dd[i], i, 1, False, False)
-                mm_g(dd[i], i, ap_q, ap_s, False, True)
+                mm_g(dd[i], i, 1)
 
-            def relu(i):
+            def pcopy(i):
                 rp[i] = work.tile([P, R], F32, name="rp", bufs=4)
-                nc.scalar.activation(out=rp[i][:], in_=pp[i][:], func=ACT.Relu)
+                nc.scalar.copy(out=rp[i][:], in_=pp[i][:])
 
-            nd = {}
-            rs = {}
-
-            def num_den(i):
-                nd[i] = work.tile([P, 2, R], F32, name="nd", bufs=4)
+            def num_(i):
                 nc.vector.scalar_tensor_tensor(
-                    out=nd[i][:, 0, :], in0=gg[i][:], scalar=1e-30, in1=rp[i][:], op0=ALU.max, op1=ALU.add
-                )
-                nc.vector.tensor_tensor(out=nd[i][:, 1, :], in0=rp[i][:], in1=dd[i][:], op=ALU.subtract)
-
-            def rsqrt(i):
-                rs[i] = work.tile([P, 2, R], F32, name="rs", bufs=4)
-                nc.scalar.activation(out=rs[i][:], in_=nd[i][:], func=ACT.Abs_reciprocal_sqrt)
-
-            def times_g(i):
-                nc.gpsimd.tensor_tensor(
-                    out=nd[i][:, 0, :], in0=nd[i][:, 0, :], in1=g_sb[i // 4][:, i % 4, :], op=ALU.mult
+                    out=num[:, i, :], in0=rp[i][:], scalar=0.0, in1=gg[i][:], op0=ALU.max, op1=ALU.add
                 )
 
-            def finish(i):
-                nc.vector.tensor_tensor(out=rs[i][:, 0, :], in0=rs[i][:, 0, :], in1=rs[i][:, 1, :], op=ALU.mult)
+            def den_(i):
+                nc.vector.scalar_tensor_tensor(
+                    out=den[:, i, :], in0=rp[i][:], scalar=0.0, in1=dd[i][:], op0=ALU.min, op1=ALU.subtract
+                )
 
-            def finish2(i):
-                res = work.tile([P, R], F32, name="res", bufs=3)
-                nc.vector.tensor_tensor(out=res[:], in0=rs[i][:, 0, :], in1=nd[i][:, 0, :], op=ALU.mult)
-                nc.sync.dma_start(out=out[i * P : (i + 1) * P, :], in_=res[:])
+            def rsqrt(i, n):
+                nc.scalar.activation(out=den[:, i : i + n, :], in_=den[:, i : i + n, :], func=ACT.Abs_reciprocal_sqrt)
 
-            interleave_f(nc.vector.tensor_copy, 0, 0, 2)
-            interleave_f(nc.vector.tensor_copy, 0, 2, 4)
-            interleave_f(nc.scalar.copy, 1, 0, 4)
-            nc.vector.scalar_tensor_tensor(out=e_neg[:], in0=c_col[:], scalar=-1.0, in1=d_col[:], op0=ALU.mult, op1=ALU.mult)
+            def sqrt(i, n):
+                nc.scalar.activation(out=num[:, i : i + n, :], in_=num[:, i : i + n, :], func=ACT.Sqrt)
+
+            def times_g(e, x, i, n):
+                mul_on[e](out=x[:, i : i + n, :], in0=x[:, i : i + n, :], in1=g_sb[i // 4][:, i % 4 : i % 4 + n, :], op=ALU.mult)
+
+            def final(i, n):
+                nc.vector.tensor_tensor(out=num[:, i : i + n, :], in0=num[:, i : i + n, :], in1=den[:, i : i + n, :], op=ALU.mult)
+                for q in range(i, i + n):
+                    nc.sync.dma_start(out=out[q * P : (q + 1) * P, :], in_=num[:, q, :])
+
+            def e_make():
+                nc.gpsimd.tensor_tensor(out=e_pos[:], in0=c_col[:], in1=d_col[:], op=ALU.mult)
+                nc.gpsimd.tensor_scalar(out=e_neg[:], in0=e_pos[:], scalar1=-1.0, scalar2=None, op0=ALU.mult)
+
+            def quant_a():
+                quant(a_q[:].rearrange("p z r -> p (z r)"), a_s[:].rearrange("p z r -> p (z r)"), a_int[:].rearrange("p z r t -> p (z r t)"))
+            e_make()
+            interleave_f('V', 0, 0, 256)
+            interleave_f('V', 0, 256, 512)
+            interleave_f('S', 1, 0, 320)
             make_fm(0)
-            quant_f(0)
-            quant_fm(0)
+            interleave_f('V', 1, 320, 512)
             make_fm(1)
-            quant_f(1)
-            quant_fm(1)
-            gain(0)
-            for k in range(G):
-                for t in range(T):
-                    widen(0, k, t)
-            a_ps = []
-            for n in range(4):
-                a_ps.append(a_chunk(n, ["pp", "gg", "dd", "pp"][n]))
-            tr00 = transpose_g(0, 0)
-            tr01 = transpose_g(0, 1)
-            interleave_x(nc.scalar.copy, 0, 1)
-            empty_g(0, 0, tr00)
-            empty_g(0, 1, tr01)
-            for n in range(4):
-                a_parts(n, a_ps[n], an_int, ALU.min)
-                a_parts(n, a_ps[n], ap_int, ALU.max)
-            for t in range(T):
-                widen(1, 0, t)
-            interleave_x(nc.vector.tensor_copy, 0, 0)
-            quant(an_q[:], an_s[:], an_int[:].rearrange("p r t -> p (r t)"))
-            quant(ap_q[:], ap_s[:], ap_int[:].rearrange("p r t -> p (r t)"))
+            quant_f()
+            quant_fm()
+            widen('S', 0, 0, 0)
+            widen('S', 0, 0, 1)
+            widen('S', 0, 0, 2)
+            widen('S', 0, 0, 3)
+            widen('S', 0, 1, 0)
+            widen('S', 0, 1, 1)
+            widen('S', 0, 1, 2)
+            widen('S', 0, 1, 3)
+            a_chunk(0, 'pp')
+            a_chunk(1, 'gg')
+            a_chunk(2, 'dd')
+            a_chunk(3, 'pp')
+            gain('V', 0)
+            gain('V', 1)
+            transpose_g(0, 0)
+            transpose_g(0, 1)
+            interleave_x('G', 0, 0, 0, 512)
+            interleave_x('G', 0, 1, 0, 512)
+            a_part(0, 0)
+            a_part(0, 1)
+            a_part(1, 0)
+            a_part(1, 1)
+            a_part(2, 0)
+            a_part(2, 1)
+            a_part(3, 0)
+            a_part(3, 1)
+            widen('S', 1, 0, 0)
+            widen('S', 1, 0, 1)
+            empty_g('S', 0, 0)
+            empty_g('S', 0, 1)
+            widen('S', 1, 0, 2)
+            widen('S', 1, 0, 3)
             quant_x(0, 0)
-            quant_g(0)
+            gain('V', 2)
             quant_x(0, 1)
-            matmuls(0)
-            relu(0)
-            gain(1)
-            for t in range(T):
-                widen(1, 1, t)
-            tr10 = transpose_g(1, 0)
-            tr11 = transpose_g(1, 1)
-            empty_g(1, 0, tr10)
-            empty_g(1, 1, tr11)
-            interleave_x(nc.vector.tensor_copy, 1, 0)
-
-            s_fill = {
-                0: [lambda: interleave_x(nc.scalar.copy, 1, 1)],
-                1: [lambda: widen(2, 0, 0)],
-                2: [lambda: widen(2, 0, 1), lambda: widen(2, 0, 2)],
-                3: [lambda: widen(2, 0, 3), lambda: widen(2, 1, 0)],
-                4: [lambda: widen(2, 1, 1), lambda: widen(2, 1, 2), lambda: widen(2, 1, 3)],
-                5: [lambda: interleave_x(nc.scalar.copy, 2, 1)],
-            }
-            v_fill = {
-                0: [lambda: quant_x(1, 0)],
-                1: [lambda: quant_g(1)],
-                2: [lambda: gain(2), lambda: quant_x(1, 1)],
-                5: [lambda: interleave_x(nc.vector.tensor_copy, 2, 0), lambda: quant_g(2)],
-                6: [lambda: quant_x(2, 0), lambda: quant_x(2, 1)],
-            }
-            tr2 = []
-            for i in range(NT):
-                if i + 1 < NT:
-                    matmuls(i + 1)
-                    relu(i + 1)
-                num_den(i)
-                for fill in s_fill.get(i, []):
-                    fill()
-                if i == 3:
-                    tr2.append(transpose_g(2, 0))
-                    tr2.append(transpose_g(2, 1))
-                if i == 4:
-                    empty_g(2, 0, tr2[0])
-                    empty_g(2, 1, tr2[1])
-                rsqrt(i)
-                if i >= 2:
-                    finish(i - 2)
-                for fill in v_fill.get(i, []):
-                    fill()
-                if i >= 2:
-                    finish2(i - 2)
-                times_g(i)
-            finish(NT - 2)
-            finish2(NT - 2)
-            finish(NT - 1)
-            finish2(NT - 1)
+            quant_g(0)
+            quant_a()
+            widen('S', 1, 1, 0)
+            widen('S', 1, 1, 1)
+            widen('S', 1, 1, 2)
+            widen('S', 1, 1, 3)
+            mm_p(0)
+            mm_n(0)
+            mm_d(0)
+            pcopy(0)
+            mm_p(1)
+            mm_n(1)
+            mm_d(1)
+            pcopy(1)
+            transpose_g(1, 0)
+            transpose_g(1, 1)
+            interleave_x('V', 1, 0, 0, 1024)
+            num_(0)
+            den_(0)
+            empty_g('S', 1, 0)
+            empty_g('S', 1, 1)
+            transpose_g(2, 0)
+            transpose_g(2, 1)
+            mm_p(2)
+            mm_n(2)
+            mm_d(2)
+            empty_g('S', 2, 0)
+            empty_g('S', 2, 1)
+            interleave_x('S', 1, 1, 512, 1024)
+            interleave_x('V', 1, 1, 0, 512)
+            num_(1)
+            den_(1)
+            quant_x(1, 0)
+            quant_g(1)
+            pcopy(2)
+            mm_p(3)
+            mm_n(3)
+            mm_d(3)
+            pcopy(3)
+            num_(2)
+            den_(2)
+            quant_x(1, 1)
+            rsqrt(0, 2)
+            times_g('G', den, 0, 1)
+            times_g('G', den, 1, 1)
+            mm_p(4)
+            mm_n(4)
+            mm_d(4)
+            pcopy(4)
+            num_(3)
+            den_(3)
+            mm_p(5)
+            mm_n(5)
+            mm_d(5)
+            pcopy(5)
+            num_(4)
+            den_(4)
+            rsqrt(2, 2)
+            times_g('G', den, 2, 1)
+            times_g('G', den, 3, 1)
+            mm_p(6)
+            mm_n(6)
+            mm_d(6)
+            pcopy(6)
+            num_(5)
+            den_(5)
+            mm_p(7)
+            mm_n(7)
+            mm_d(7)
+            pcopy(7)
+            num_(6)
+            den_(6)
+            rsqrt(4, 2)
+            times_g('G', den, 4, 1)
+            times_g('G', den, 5, 1)
+            mm_p(8)
+            pcopy(8)
+            mm_n(8)
+            mm_d(8)
+            num_(7)
+            den_(7)
+            mm_p(9)
+            pcopy(9)
+            mm_n(9)
+            mm_d(9)
+            rsqrt(6, 2)
+            times_g('G', den, 6, 1)
+            times_g('G', den, 7, 1)
+            mm_p(10)
+            pcopy(10)
+            num_(8)
+            den_(8)
+            mm_n(10)
+            mm_d(10)
+            mm_p(11)
+            pcopy(11)
+            num_(9)
+            den_(9)
+            sqrt(0, 2)
+            num_(10)
+            den_(10)
+            mm_n(11)
+            mm_d(11)
+            sqrt(2, 2)
+            num_(11)
+            den_(11)
+            final(0, 2)
+            sqrt(8, 2)
+            final(2, 2)
+            times_g('V', num, 8, 2)
+            sqrt(10, 2)
+            times_g('V', num, 10, 2)
+            sqrt(4, 2)
+            final(4, 2)
+            sqrt(6, 2)
+            final(6, 2)
+            rsqrt(8, 2)
+            rsqrt(10, 1)
+            final(8, 2)
+            rsqrt(11, 1)
+            final(10, 1)
+            final(11, 1)

@@ -244,7 +244,7 @@ def tile_seminmfsquarerootupdate_kernel(tc, x_bytes, x_scale, f, g, m, c, d, out
                 mm_g(dd[i], i, 1)
 
             def pcopy(i):
-                rp[i] = work.tile([P, R], F32, name="rp", bufs=4)
+                rp[i] = work.tile([P, R], F32, name="rp", bufs=6)
                 nc.scalar.copy(out=rp[i][:], in_=pp[i][:])
 
             def num_(i):
@@ -281,8 +281,8 @@ def tile_seminmfsquarerootupdate_kernel(tc, x_bytes, x_scale, f, g, m, c, d, out
             interleave_f('V', 0, 0, 256)
             interleave_f('V', 0, 256, 512)
             interleave_f('S', 1, 0, 320)
-            make_fm(0)
             interleave_f('V', 1, 320, 512)
+            make_fm(0)
             make_fm(1)
             quant_f()
             quant_fm()
@@ -299,11 +299,9 @@ def tile_seminmfsquarerootupdate_kernel(tc, x_bytes, x_scale, f, g, m, c, d, out
             a_chunk(2, 'dd')
             a_chunk(3, 'pp')
             gain('V', 0)
-            gain('V', 1)
+            interleave_x('V', 0, 0, 0, 512)
             transpose_g(0, 0)
             transpose_g(0, 1)
-            interleave_x('G', 0, 0, 0, 512)
-            interleave_x('G', 0, 1, 0, 512)
             a_part(0, 0)
             a_part(0, 1)
             a_part(1, 0)
@@ -313,133 +311,135 @@ def tile_seminmfsquarerootupdate_kernel(tc, x_bytes, x_scale, f, g, m, c, d, out
             a_part(3, 0)
             a_part(3, 1)
             widen('S', 1, 0, 0)
-            widen('S', 1, 0, 1)
             empty_g('S', 0, 0)
+            widen('S', 1, 0, 1)
             empty_g('S', 0, 1)
             widen('S', 1, 0, 2)
             widen('S', 1, 0, 3)
-            quant_x(0, 0)
-            gain('V', 2)
-            quant_x(0, 1)
-            quant_g(0)
-            quant_a()
-            widen('S', 1, 1, 0)
-            widen('S', 1, 1, 1)
-            widen('S', 1, 1, 2)
-            widen('S', 1, 1, 3)
-            mm_p(0)
-            mm_n(0)
-            mm_d(0)
-            pcopy(0)
-            mm_p(1)
-            mm_n(1)
-            mm_d(1)
-            pcopy(1)
+            gain('V', 1)
             transpose_g(1, 0)
             transpose_g(1, 1)
-            interleave_x('V', 1, 0, 0, 1024)
-            num_(0)
-            den_(0)
+            interleave_x('V', 0, 1, 0, 512)
+            quant_x(0, 0)
+            quant_a()
+            quant_g(0)
+            quant_x(0, 1)
+            gain('V', 2)
+            widen('S', 1, 1, 0)
             empty_g('S', 1, 0)
             empty_g('S', 1, 1)
             transpose_g(2, 0)
             transpose_g(2, 1)
+            widen('S', 1, 1, 1)
+            widen('S', 1, 1, 2)
+            widen('S', 1, 1, 3)
+            mm_p(0)
+            mm_p(1)
+            mm_n(0)
+            mm_d(0)
+            mm_n(1)
+            mm_d(1)
+            interleave_x('V', 1, 0, 0, 1024)
+            interleave_x('S', 1, 1, 0, 768)
+            interleave_x('V', 1, 1, 768, 1024)
+            pcopy(0)
+            pcopy(1)
             mm_p(2)
-            mm_n(2)
-            mm_d(2)
+            mm_p(3)
+            quant_x(1, 0)
+            num_(0)
+            den_(0)
             empty_g('S', 2, 0)
             empty_g('S', 2, 1)
-            interleave_x('S', 1, 1, 512, 1024)
-            interleave_x('V', 1, 1, 0, 512)
+            quant_x(1, 1)
+            pcopy(2)
+            pcopy(3)
+            mm_p(4)
+            mm_p(5)
             num_(1)
             den_(1)
-            quant_x(1, 0)
-            quant_g(1)
-            pcopy(2)
-            mm_p(3)
+            mm_n(2)
+            mm_d(2)
             mm_n(3)
             mm_d(3)
-            pcopy(3)
+            quant_g(1)
+            pcopy(4)
+            rsqrt(0, 2)
             num_(2)
             den_(2)
-            quant_x(1, 1)
-            rsqrt(0, 2)
             times_g('G', den, 0, 1)
-            times_g('G', den, 1, 1)
-            mm_p(4)
-            mm_n(4)
-            mm_d(4)
-            pcopy(4)
             num_(3)
             den_(3)
-            mm_p(5)
+            times_g('G', den, 1, 1)
+            pcopy(5)
+            mm_n(4)
+            mm_d(4)
+            mm_p(6)
             mm_n(5)
             mm_d(5)
-            pcopy(5)
+            mm_p(7)
+            rsqrt(2, 2)
             num_(4)
             den_(4)
-            rsqrt(2, 2)
             times_g('G', den, 2, 1)
-            times_g('G', den, 3, 1)
-            mm_p(6)
+            pcopy(6)
             mm_n(6)
             mm_d(6)
-            pcopy(6)
             num_(5)
             den_(5)
-            mm_p(7)
+            times_g('G', den, 3, 1)
+            pcopy(7)
             mm_n(7)
             mm_d(7)
-            pcopy(7)
+            rsqrt(4, 2)
             num_(6)
             den_(6)
-            rsqrt(4, 2)
             times_g('G', den, 4, 1)
-            times_g('G', den, 5, 1)
             mm_p(8)
             pcopy(8)
-            mm_n(8)
-            mm_d(8)
             num_(7)
             den_(7)
+            times_g('G', den, 5, 1)
+            mm_n(8)
+            mm_d(8)
             mm_p(9)
             pcopy(9)
+            rsqrt(6, 2)
             mm_n(9)
             mm_d(9)
-            rsqrt(6, 2)
-            times_g('G', den, 6, 1)
-            times_g('G', den, 7, 1)
             mm_p(10)
             pcopy(10)
+            times_g('G', den, 6, 1)
             num_(8)
             den_(8)
+            times_g('G', den, 7, 1)
             mm_n(10)
             mm_d(10)
             mm_p(11)
             pcopy(11)
             num_(9)
             den_(9)
-            sqrt(0, 2)
-            num_(10)
-            den_(10)
             mm_n(11)
             mm_d(11)
-            sqrt(2, 2)
+            rsqrt(8, 2)
+            num_(10)
+            den_(10)
+            sqrt(0, 2)
             num_(11)
             den_(11)
+            times_g('V', den, 8, 2)
             final(0, 2)
-            sqrt(8, 2)
+            sqrt(2, 2)
             final(2, 2)
-            times_g('V', num, 8, 2)
             sqrt(10, 2)
-            times_g('V', num, 10, 2)
             sqrt(4, 2)
+            times_g('V', num, 10, 2)
             final(4, 2)
             sqrt(6, 2)
             final(6, 2)
-            rsqrt(8, 2)
-            rsqrt(10, 1)
+            sqrt(8, 2)
             final(8, 2)
-            rsqrt(11, 1)
+            rsqrt(10, 1)
             final(10, 1)
+            rsqrt(11, 1)
             final(11, 1)

@@ -3,7 +3,7 @@ from contextlib import ExitStack
 import concourse.mybir as mybir
 from concourse.masks import make_identity
 
-M, N, R = 1024, 1536, 512
+SAMPLES, N, R = 1024, 1536, 512
 
 F32 = mybir.dt.float32
 BF16 = mybir.dt.bfloat16
@@ -15,431 +15,407 @@ ALU = mybir.AluOpType
 ACT = mybir.ActivationFunctionType
 
 P = 128
-G = 2
-T = 4
-NT = N // P
+PACK = 4
+PASSES = SAMPLES // (P * PACK)
+TILES = N // P
+LOAD_TILES = 4
+LOADS = TILES // LOAD_TILES
 CHUNKS = ((0, 512), (512, 1024))
+F_SCALAR = 320
+X_SCALAR = 768
 
-FLOPS = 2 * N * R * M + 2 * R * R * M + 2 * 2 * N * R * R
+FLOPS = 2 * N * R * SAMPLES + 2 * R * R * SAMPLES + 2 * 2 * N * R * R
 
 
 def tile_seminmfsquarerootupdate_kernel(tc, x_bytes, x_scale, f, g, m, c, d, out):
     nc = tc.nc
     with ExitStack() as ctx:
-        const = ctx.enter_context(tc.tile_pool(name="const", bufs=1))
+        keep = ctx.enter_context(tc.tile_pool(name="keep", bufs=1))
         work = ctx.enter_context(tc.tile_pool(name="work", bufs=2))
         psum = ctx.enter_context(tc.psum_pool(name="psum", bufs=2))
 
-        ident = const.tile([P, P], F32, name="ident")
-        warm = const.tile([P, 1], F32, name="warm")
-        warm2 = const.tile([P, 1], F32, name="warm2")
-        m_sb = const.tile([P, G, T], BF16, name="m_sb")
-        xs_sb = const.tile([P, G, T], F32, name="xs_sb")
-        c_row = const.tile([P, R], BF16, name="c_row")
-        c_col = const.tile([P, T], BF16, name="c_col")
-        d_col = const.tile([P, T], BF16, name="d_col")
-        e_neg = const.tile([P, T], F32, name="e_neg")
-        e_pos = const.tile([P, T], F32, name="e_pos")
+        ident = keep.tile([P, P], F32, name="ident")
+        table_in = keep.tile([P, 1], F32, name="table_in")
+        table_out = keep.tile([P, 1], F32, name="table_out")
+        m_sb = keep.tile([P, PASSES, PACK], BF16, name="m_sb")
+        x_scale_sb = keep.tile([P, PASSES, PACK], F32, name="x_scale_sb")
+        c_row = keep.tile([P, R], BF16, name="c_row")
+        c_col = keep.tile([P, PACK], BF16, name="c_col")
+        d_col = keep.tile([P, PACK], BF16, name="d_col")
+        e_minus = keep.tile([P, PACK], F32, name="e_minus")
+        e_plus = keep.tile([P, PACK], F32, name="e_plus")
 
-        f_raw = [const.tile([P, T, R], BF16, name="f_raw%d" % k, align_bytes=64) for k in range(G)]
-        f_int = const.tile([P, G, T, P, T], BF16, name="f_int", align_bytes=64)
-        fm_int = const.tile([P, G, R, T], BF16, name="fm_int", align_bytes=64)
-        f_q = const.tile([P, G, R], U32, name="f_q", align_bytes=64)
-        f_s = const.tile([P, G, R], U8, name="f_s", align_bytes=64)
-        fm_q = const.tile([P, G, R], U32, name="fm_q", align_bytes=64)
-        fm_s = const.tile([P, G, R], U8, name="fm_s", align_bytes=64)
-        xb = {}
-        for k in range(G):
-            for h in range(2):
-                xb[k, h] = const.tile([P, 2, N], U8, name="xb%d%d" % (k, h), align_bytes=64)
-        x_q = {}
-        x_s = {}
-        x_w = {}
-        x_i = {}
-        g_q = []
-        g_s = []
-        g_i = []
-        for ch, (lo, w) in enumerate(CHUNKS):
-            for k in range(G):
-                x_w[ch, k] = const.tile([P, T, w], BF16, name="x_w%d%d" % (ch, k), align_bytes=64)
-                x_i[ch, k] = const.tile([P, w, T], BF16, name="x_i%d%d" % (ch, k), align_bytes=64)
-                x_q[ch, k] = const.tile([P, w], U32, name="x_q%d%d" % (ch, k), align_bytes=64)
-                x_s[ch, k] = const.tile([P, w], U8, name="x_s%d%d" % (ch, k), align_bytes=64)
-            g_q.append(const.tile([P, w], U32, name="g_q%d" % ch, align_bytes=64))
-            g_s.append(const.tile([P, w], U8, name="g_s%d" % ch, align_bytes=64))
-            g_i.append(const.tile([P, w, T], BF16, name="g_i%d" % ch, align_bytes=64))
-        g_sb = [const.tile([P, 4, R], BF16, name="g_sb%d" % h, align_bytes=64) for h in range(3)]
-        a_int = const.tile([P, 2, R, T], BF16, name="a_int", align_bytes=64)
-        a_q = const.tile([P, 2, R], U32, name="a_q", align_bytes=64)
-        a_s = const.tile([P, 2, R], U8, name="a_s", align_bytes=64)
-        num = const.tile([P, NT, R], F32, name="num")
-        den = const.tile([P, NT, R], F32, name="den")
+        f_rows = [keep.tile([P, PACK, R], BF16, name="f_rows%d" % k, align_bytes=64) for k in range(PASSES)]
+        f_inter = keep.tile([P, PASSES, PACK, P, PACK], BF16, name="f_inter", align_bytes=64)
+        fm_inter = keep.tile([P, PASSES, R, PACK], BF16, name="fm_inter", align_bytes=64)
+        f_codes = keep.tile([P, PASSES, R], U32, name="f_codes", align_bytes=64)
+        f_scales = keep.tile([P, PASSES, R], U8, name="f_scales", align_bytes=64)
+        fm_codes = keep.tile([P, PASSES, R], U32, name="fm_codes", align_bytes=64)
+        fm_scales = keep.tile([P, PASSES, R], U8, name="fm_scales", align_bytes=64)
 
-        f_v = f.rearrange("(k p t) r -> k p t r", p=P, t=T)
-        x_v = x_bytes.rearrange("(k p t) n -> k p t n", p=P, t=T)
-        g_v = g.rearrange("(h i p) r -> h p i r", i=4, p=P)
+        x_raw = {}
+        for k in range(PASSES):
+            for half in range(2):
+                x_raw[k, half] = keep.tile([P, 2, N], U8, name="x_raw%d%d" % (k, half), align_bytes=64)
+        x_rows = {}
+        x_inter = {}
+        x_codes = {}
+        x_scales = {}
+        gc_inter = []
+        gc_codes = []
+        gc_scales = []
+        for ch, (first, width) in enumerate(CHUNKS):
+            for k in range(PASSES):
+                x_rows[ch, k] = keep.tile([P, PACK, width], BF16, name="x_rows%d%d" % (ch, k), align_bytes=64)
+                x_inter[ch, k] = keep.tile([P, width, PACK], BF16, name="x_inter%d%d" % (ch, k), align_bytes=64)
+                x_codes[ch, k] = keep.tile([P, width], U32, name="x_codes%d%d" % (ch, k), align_bytes=64)
+                x_scales[ch, k] = keep.tile([P, width], U8, name="x_scales%d%d" % (ch, k), align_bytes=64)
+            gc_codes.append(keep.tile([P, width], U32, name="gc_codes%d" % ch, align_bytes=64))
+            gc_scales.append(keep.tile([P, width], U8, name="gc_scales%d" % ch, align_bytes=64))
+            gc_inter.append(keep.tile([P, width, PACK], BF16, name="gc_inter%d" % ch, align_bytes=64))
+        g_sb = [keep.tile([P, LOAD_TILES, R], BF16, name="g_sb%d" % h, align_bytes=64) for h in range(LOADS)]
+        a_inter = keep.tile([P, 2, R, PACK], BF16, name="a_inter", align_bytes=64)
+        a_codes = keep.tile([P, 2, R], U32, name="a_codes", align_bytes=64)
+        a_scales = keep.tile([P, 2, R], U8, name="a_scales", align_bytes=64)
+        num = keep.tile([P, TILES, R], F32, name="num")
+        den = keep.tile([P, TILES, R], F32, name="den")
 
-        with tc.manual_schedule():
-            nc.scalar.dma_start(out=m_sb[:], in_=m.rearrange("(k p t) -> p k t", p=P, t=T))
-            nc.scalar.dma_start(out=xs_sb[:], in_=x_scale.rearrange("(k p t) o -> p k (t o)", p=P, t=T))
-            nc.gpsimd.dma_start(out=c_row[:], in_=c.partition_broadcast(P))
-            nc.gpsimd.dma_start(out=c_col[:], in_=c.rearrange("(p t) -> p t", t=T))
-            nc.gpsimd.dma_start(out=d_col[:], in_=d.rearrange("(p t) -> p t", t=T))
-            for h in range(2):
-                nc.sync.dma_start(out=f_raw[0][:, :, h * 256 : (h + 1) * 256], in_=f_v[0, :, :, h * 256 : (h + 1) * 256])
-            nc.sync.dma_start(out=f_raw[1][:], in_=f_v[1])
-            for h in range(2):
-                nc.sync.dma_start(out=xb[0, h][:], in_=x_v[0, :, 2 * h : 2 * h + 2, :])
-            nc.sync.dma_start(out=g_sb[0][:], in_=g_v[0])
-            for h in range(2):
-                nc.sync.dma_start(out=xb[1, h][:], in_=x_v[1, :, 2 * h : 2 * h + 2, :])
-            for h in range(1, 3):
-                nc.sync.dma_start(out=g_sb[h][:], in_=g_v[h])
-            nc.vector.memset(warm[:], 1.0)
-            nc.scalar.activation(out=warm2[:], in_=warm[:], func=ACT.Abs_reciprocal_sqrt)
-            make_identity(nc, ident[:])
+        f_view = f.rearrange("(k q t) r -> k q t r", q=P, t=PACK)
+        x_view = x_bytes.rearrange("(k q t) n -> k q t n", q=P, t=PACK)
+        g_view = g.rearrange("(h i q) r -> h q i r", i=LOAD_TILES, q=P)
 
-            copy_on = {"V": nc.vector.tensor_copy, "S": nc.scalar.copy}
-            mul_on = {"V": nc.vector.tensor_tensor, "G": nc.gpsimd.tensor_tensor}
+        def vector_copy(dst, src):
+            nc.vector.tensor_copy(out=dst, in_=src)
 
-            def copy(e, dst, src):
-                if e == "G":
-                    nc.gpsimd.tensor_scalar(out=dst, in0=src, scalar1=1.0, scalar2=0.0, op0=ALU.mult, op1=ALU.add)
-                else:
-                    copy_on[e](out=dst, in_=src)
+        def scalar_copy(dst, src):
+            nc.scalar.copy(out=dst, in_=src)
 
-            def interleave_f(e, k, lo, hi):
-                copy(e, f_int[:, k, :, lo // 4 : hi // 4, :], f_raw[k][:, :, lo:hi].rearrange("p j (q t) -> p t q j", t=T))
+        def quantize(codes, scales, values):
+            nc.vector.quantize_mx(out=codes.bitcast(FP8X4), scales=scales, in_=values)
 
-            def make_fm(k):
-                nc.vector.tensor_tensor(
-                    out=fm_int[:, k, :, :].rearrange("p (q t) j -> p q t j", t=T),
-                    in0=f_int[:, k, :, :, :].rearrange("p t q j -> p q t j"),
-                    in1=m_sb[:, k, :].unsqueeze(1).unsqueeze(1).to_broadcast([P, P, T, T]),
-                    op=ALU.mult,
-                )
+        def interleave_f(copy, k, lo, hi):
+            copy(
+                f_inter[:, k, :, lo // PACK : hi // PACK, :],
+                f_rows[k][:, :, lo:hi].rearrange("p j (q t) -> p t q j", t=PACK),
+            )
 
-            def quant(codes, scales, src):
-                nc.vector.quantize_mx(out=codes.bitcast(FP8X4), scales=scales, in_=src)
+        def weight_f(k):
+            nc.vector.tensor_tensor(
+                out=fm_inter[:, k, :, :].rearrange("p (q t) j -> p q t j", t=PACK),
+                in0=f_inter[:, k, :, :, :].rearrange("p t q j -> p q t j"),
+                in1=m_sb[:, k, :].unsqueeze(1).unsqueeze(1).to_broadcast([P, P, PACK, PACK]),
+                op=ALU.mult,
+            )
 
-            def quant_f():
-                quant(f_q[:].rearrange("p k r -> p (k r)"), f_s[:].rearrange("p k r -> p (k r)"), f_int[:].rearrange("p k t q j -> p (k t q j)"))
+        def scale_x(ch, k, t):
+            first, width = CHUNKS[ch]
+            nc.scalar.activation(
+                out=x_rows[ch, k][:, t, :],
+                in_=x_raw[k, t // 2][:, t % 2, first : first + width].bitcast(FP8),
+                func=ACT.Copy,
+                scale=x_scale_sb[:, k, t : t + 1],
+            )
 
-            def quant_fm():
-                quant(fm_q[:].rearrange("p k r -> p (k r)"), fm_s[:].rearrange("p k r -> p (k r)"), fm_int[:].rearrange("p k r j -> p (k r j)"))
+        def interleave_x(copy, ch, k, lo, hi):
+            copy(
+                x_inter[ch, k][:, lo:hi, :].rearrange("p (n i) t -> p n t i", i=4),
+                x_rows[ch, k][:, :, lo:hi].rearrange("p t (n i) -> p n t i", i=4),
+            )
 
-            def widen(e, ch, k, t):
-                lo, w = CHUNKS[ch]
-                src = xb[k, t // 2][:, t % 2, lo : lo + w].bitcast(FP8)
-                if e == "S":
-                    nc.scalar.activation(out=x_w[ch, k][:, t, :], in_=src, func=ACT.Copy, scale=xs_sb[:, k, t : t + 1])
-                else:
-                    nc.vector.tensor_scalar(out=x_w[ch, k][:, t, :], in0=src, scalar1=xs_sb[:, k, t : t + 1], scalar2=None, op0=ALU.mult)
+        def quantize_x(ch, k):
+            quantize(x_codes[ch, k][:], x_scales[ch, k][:], x_inter[ch, k][:].rearrange("p n t -> p (n t)"))
 
-            def interleave_x(e, ch, k, lo, hi):
-                dst = x_i[ch, k][:, lo:hi, :]
-                src = x_w[ch, k][:, :, lo:hi]
-                if e == "G":
-                    copy(e, dst, src.rearrange("p t c -> p c t"))
-                else:
-                    copy(e, dst.rearrange("p (c i) t -> p c t i", i=4), src.rearrange("p t (c i) -> p c t i", i=4))
+        gc_rows = {}
+        gc_turned = {}
 
-            def quant_x(ch, k):
-                quant(x_q[ch, k][:], x_s[ch, k][:], x_i[ch, k][:].rearrange("p c t -> p (c t)"))
+        def gain_g(h):
+            gc_rows[h] = work.tile([P, LOAD_TILES, R], BF16, name="gc_rows", align_bytes=64)
+            nc.vector.tensor_tensor(
+                out=gc_rows[h][:],
+                in0=g_sb[h][:],
+                in1=c_row[:].unsqueeze(1).to_broadcast([P, LOAD_TILES, R]),
+                op=ALU.mult,
+            )
 
-            gc = {}
-            trs = {}
+        def turn_g(h, pair):
+            bank = psum.tile([P, 2, 2, P], F32, name="turn", tag="turn", bufs=2)
+            for i in range(2):
+                words = gc_rows[h][:, 2 * pair + i, :].bitcast(F32)
+                for u in range(2):
+                    nc.tensor.transpose(bank[:, i, u, :], words[:, u : R // 2 : 2], ident[:])
+            gc_turned[h, pair] = bank
 
-            def gain(e, h):
-                gc[h] = work.tile([P, 4, R], BF16, name="gc", align_bytes=64, bufs=2)
-                mul_on[e](out=gc[h][:], in0=g_sb[h][:], in1=c_row[:].unsqueeze(1).to_broadcast([P, 4, R]), op=ALU.mult)
+        def store_turned_g(h, pair):
+            ch = 0 if h == 0 else 1
+            words = gc_inter[ch][:].rearrange("p r t -> p (r t)").bitcast(F32)
+            start = 2 * ((2 * h + pair) * 2 * P - CHUNKS[ch][0])
+            scalar_copy(
+                words[:, start : start + 4 * P].rearrange("p (i r u) -> p i r u", i=2, u=2),
+                gc_turned[h, pair][:].rearrange("p i u r -> p i r u"),
+            )
 
-            def transpose_g(h, b):
-                tr = psum.tile([P, 2, 2, P], F32, name="tr", tag="tr", bufs=2)
-                for i in range(2):
-                    words = gc[h][:, 2 * b + i, :].bitcast(F32)
-                    for u in range(2):
-                        nc.tensor.transpose(tr[:, i, u, :], words[:, u : R // 2 : 2], ident[:])
-                trs[h, b] = tr
+        def quantize_gc(ch):
+            quantize(gc_codes[ch][:], gc_scales[ch][:], gc_inter[ch][:].rearrange("p r t -> p (r t)"))
 
-            def empty_g(e, h, b):
-                ch = min(h, 1)
-                words = g_i[ch][:].rearrange("p r t -> p (r t)").bitcast(F32)
-                o = (h * 2 + b) * 512 - 2 * CHUNKS[ch][0]
-                copy(e, words[:, o : o + 512].rearrange("p (i r u) -> p i r u", i=2, u=2), trs[h, b][:].rearrange("p i u r -> p i r u"))
+        a_banks = {}
 
-            def quant_g(ch):
-                quant(g_q[ch][:], g_s[ch][:], g_i[ch][:].rearrange("p r t -> p (r t)"))
+        def multiply_a(n, tag):
+            bank = psum.tile([P, PACK, P], F32, name="a_bank%d" % n, tag=tag, bufs=2)
+            for t in range(PACK):
+                for k in range(PASSES):
+                    nc.tensor.matmul_mx(
+                        out=bank[:, t, :],
+                        lhsT=f_codes[:, k, t * P : (t + 1) * P].bitcast(FP8X4),
+                        lhsT_scale=f_scales[:, k, t * P : (t + 1) * P],
+                        rhs=fm_codes[:, k, n * P : (n + 1) * P].bitcast(FP8X4),
+                        rhs_scale=fm_scales[:, k, n * P : (n + 1) * P],
+                        start=(k == 0),
+                        stop=(k == PASSES - 1),
+                    )
+            a_banks[n] = bank
 
-            a_ps = {}
-
-            def a_chunk(n, tag):
-                ps = psum.tile([P, T, P], F32, name="a_ps%d" % n, tag=tag, bufs=2)
-                for t in range(T):
-                    for k in range(G):
-                        nc.tensor.matmul_mx(
-                            out=ps[:, t, :],
-                            lhsT=f_q[:, k, t * P : (t + 1) * P].bitcast(FP8X4),
-                            lhsT_scale=f_s[:, k, t * P : (t + 1) * P],
-                            rhs=fm_q[:, k, n * P : (n + 1) * P].bitcast(FP8X4),
-                            rhs_scale=fm_s[:, k, n * P : (n + 1) * P],
-                            start=(k == 0),
-                            stop=(k == G - 1),
-                        )
-                a_ps[n] = ps
-
-            def a_part(n, z):
-                e, op = ((e_neg, ALU.min), (e_pos, ALU.max))[z]
+        def split_a(n):
+            for part, (op, e) in enumerate(((ALU.min, e_minus), (ALU.max, e_plus))):
                 nc.vector.scalar_tensor_tensor(
-                    out=a_int[:, z, n * P : (n + 1) * P, :],
-                    in0=a_ps[n][:].rearrange("p t n -> p n t"),
+                    out=a_inter[:, part, n * P : (n + 1) * P, :],
+                    in0=a_banks[n][:].rearrange("p t n -> p n t"),
                     scalar=0.0,
-                    in1=e[:].unsqueeze(1).to_broadcast([P, P, T]),
+                    in1=e[:].unsqueeze(1).to_broadcast([P, P, PACK]),
                     op0=op,
                     op1=ALU.mult,
                 )
 
-            pp = {}
-            gg = {}
-            dd = {}
-            rp = {}
+        p_banks = {}
+        p_sb = {}
+        gn_banks = {}
+        gp_banks = {}
 
-            def chunk_of(i):
-                for ch, (lo, w) in enumerate(CHUNKS):
-                    if lo <= i * P < lo + w:
-                        return ch, i * P - lo
+        def place(i):
+            ch = 0 if i * P < CHUNKS[0][1] else 1
+            return ch, i * P - CHUNKS[ch][0]
 
-            def mm_p(i):
-                pp[i] = psum.tile([P, R], F32, name="pp", tag="pp", bufs=2)
-                ch, o = chunk_of(i)
-                for k in range(G):
-                    nc.tensor.matmul_mx(
-                        out=pp[i][:],
-                        lhsT=x_q[ch, k][:, o : o + P].bitcast(FP8X4),
-                        lhsT_scale=x_s[ch, k][:, o : o + P],
-                        rhs=fm_q[:, k, :].bitcast(FP8X4),
-                        rhs_scale=fm_s[:, k, :],
-                        start=(k == 0),
-                        stop=(k == G - 1),
-                    )
-
-            def mm_g(ps, i, z):
-                ch, o = chunk_of(i)
+        def multiply_p(i):
+            p_banks[i] = psum.tile([P, R], F32, name="p_bank", tag="p", bufs=2)
+            ch, o = place(i)
+            for k in range(PASSES):
                 nc.tensor.matmul_mx(
-                    out=ps[:],
-                    lhsT=g_q[ch][:, o : o + P].bitcast(FP8X4),
-                    lhsT_scale=g_s[ch][:, o : o + P],
-                    rhs=a_q[:, z, :].bitcast(FP8X4),
-                    rhs_scale=a_s[:, z, :],
-                    start=True,
-                    stop=True,
+                    out=p_banks[i][:],
+                    lhsT=x_codes[ch, k][:, o : o + P].bitcast(FP8X4),
+                    lhsT_scale=x_scales[ch, k][:, o : o + P],
+                    rhs=fm_codes[:, k, :].bitcast(FP8X4),
+                    rhs_scale=fm_scales[:, k, :],
+                    start=(k == 0),
+                    stop=(k == PASSES - 1),
                 )
 
-            def mm_n(i):
-                gg[i] = psum.tile([P, R], F32, name="gg", tag="gg", bufs=2)
-                mm_g(gg[i], i, 0)
+        def multiply_gc(bank, i, part):
+            ch, o = place(i)
+            nc.tensor.matmul_mx(
+                out=bank[:],
+                lhsT=gc_codes[ch][:, o : o + P].bitcast(FP8X4),
+                lhsT_scale=gc_scales[ch][:, o : o + P],
+                rhs=a_codes[:, part, :].bitcast(FP8X4),
+                rhs_scale=a_scales[:, part, :],
+                start=True,
+                stop=True,
+            )
 
-            def mm_d(i):
-                dd[i] = psum.tile([P, R], F32, name="dd", tag="dd", bufs=2)
-                mm_g(dd[i], i, 1)
+        def multiply_gn(i, tag="gn"):
+            gn_banks[i] = psum.tile([P, R], F32, name="gn_bank", tag=tag, bufs=2)
+            multiply_gc(gn_banks[i], i, 0)
 
-            def pcopy(i):
-                rp[i] = work.tile([P, R], F32, name="rp", bufs=6)
-                nc.scalar.copy(out=rp[i][:], in_=pp[i][:])
+        def multiply_gp(i):
+            gp_banks[i] = psum.tile([P, R], F32, name="gp_bank", tag="gp", bufs=2)
+            multiply_gc(gp_banks[i], i, 1)
 
-            def num_(i):
-                nc.vector.scalar_tensor_tensor(
-                    out=num[:, i, :], in0=rp[i][:], scalar=0.0, in1=gg[i][:], op0=ALU.max, op1=ALU.add
-                )
+        def copy_p(i):
+            p_sb[i] = work.tile([P, R], F32, name="p_sb", bufs=8)
+            scalar_copy(p_sb[i][:], p_banks[i][:])
 
-            def den_(i):
-                nc.vector.scalar_tensor_tensor(
-                    out=den[:, i, :], in0=rp[i][:], scalar=0.0, in1=dd[i][:], op0=ALU.min, op1=ALU.subtract
-                )
+        def numerator(i):
+            nc.vector.scalar_tensor_tensor(
+                out=num[:, i, :], in0=p_sb[i][:], scalar=0.0, in1=gn_banks[i][:], op0=ALU.max, op1=ALU.add
+            )
 
-            def rsqrt(i, n):
-                nc.scalar.activation(out=den[:, i : i + n, :], in_=den[:, i : i + n, :], func=ACT.Abs_reciprocal_sqrt)
+        def denominator(i):
+            nc.vector.scalar_tensor_tensor(
+                out=den[:, i, :], in0=p_sb[i][:], scalar=0.0, in1=gp_banks[i][:], op0=ALU.min, op1=ALU.subtract
+            )
 
-            def sqrt(i, n):
-                nc.scalar.activation(out=num[:, i : i + n, :], in_=num[:, i : i + n, :], func=ACT.Sqrt)
+        def root_num(i):
+            nc.scalar.activation(out=num[:, i : i + 2, :], in_=num[:, i : i + 2, :], func=ACT.Sqrt)
 
-            def times_g(e, x, i, n):
-                mul_on[e](out=x[:, i : i + n, :], in0=x[:, i : i + n, :], in1=g_sb[i // 4][:, i % 4 : i % 4 + n, :], op=ALU.mult)
+        def root_den(i, tiles, lo=0, hi=R):
+            window = den[:, i : i + tiles, lo:hi]
+            nc.scalar.activation(out=window, in_=window, func=ACT.Abs_reciprocal_sqrt)
 
-            def final(i, n):
-                nc.vector.tensor_tensor(out=num[:, i : i + n, :], in0=num[:, i : i + n, :], in1=den[:, i : i + n, :], op=ALU.mult)
-                for q in range(i, i + n):
-                    nc.sync.dma_start(out=out[q * P : (q + 1) * P, :], in_=num[:, q, :])
+        def times_g(multiply, i, tiles):
+            o = i % LOAD_TILES
+            window = num[:, i : i + tiles, :]
+            multiply(out=window, in0=window, in1=g_sb[i // LOAD_TILES][:, o : o + tiles, :], op=ALU.mult)
 
-            def e_make():
-                nc.gpsimd.tensor_tensor(out=e_pos[:], in0=c_col[:], in1=d_col[:], op=ALU.mult)
-                nc.gpsimd.tensor_scalar(out=e_neg[:], in0=e_pos[:], scalar1=-1.0, scalar2=None, op0=ALU.mult)
+        def finish(i, tiles, lo=0, hi=R):
+            window = num[:, i : i + tiles, lo:hi]
+            nc.vector.tensor_tensor(out=window, in0=window, in1=den[:, i : i + tiles, lo:hi], op=ALU.mult)
+            for tile in range(i, i + tiles):
+                nc.sync.dma_start(out=out[tile * P : (tile + 1) * P, lo:hi], in_=num[:, tile, lo:hi])
 
-            def quant_a():
-                quant(a_q[:].rearrange("p z r -> p (z r)"), a_s[:].rearrange("p z r -> p (z r)"), a_int[:].rearrange("p z r t -> p (z r t)"))
-            e_make()
-            interleave_f('V', 0, 0, 256)
-            interleave_f('V', 0, 256, 512)
-            interleave_f('S', 1, 0, 320)
-            interleave_f('V', 1, 320, 512)
-            make_fm(0)
-            make_fm(1)
-            quant_f()
-            quant_fm()
-            widen('S', 0, 0, 0)
-            widen('S', 0, 0, 1)
-            widen('S', 0, 0, 2)
-            widen('S', 0, 0, 3)
-            widen('S', 0, 1, 0)
-            widen('S', 0, 1, 1)
-            widen('S', 0, 1, 2)
-            widen('S', 0, 1, 3)
-            a_chunk(0, 'pp')
-            a_chunk(1, 'gg')
-            a_chunk(2, 'dd')
-            a_chunk(3, 'pp')
-            gain('V', 0)
-            interleave_x('V', 0, 0, 0, 512)
-            transpose_g(0, 0)
-            transpose_g(0, 1)
-            a_part(0, 0)
-            a_part(0, 1)
-            a_part(1, 0)
-            a_part(1, 1)
-            a_part(2, 0)
-            a_part(2, 1)
-            a_part(3, 0)
-            a_part(3, 1)
-            widen('S', 1, 0, 0)
-            empty_g('S', 0, 0)
-            widen('S', 1, 0, 1)
-            empty_g('S', 0, 1)
-            widen('S', 1, 0, 2)
-            widen('S', 1, 0, 3)
-            gain('V', 1)
-            transpose_g(1, 0)
-            transpose_g(1, 1)
-            interleave_x('V', 0, 1, 0, 512)
-            quant_x(0, 0)
-            quant_a()
-            quant_g(0)
-            quant_x(0, 1)
-            gain('V', 2)
-            widen('S', 1, 1, 0)
-            empty_g('S', 1, 0)
-            empty_g('S', 1, 1)
-            transpose_g(2, 0)
-            transpose_g(2, 1)
-            widen('S', 1, 1, 1)
-            widen('S', 1, 1, 2)
-            widen('S', 1, 1, 3)
-            mm_p(0)
-            mm_p(1)
-            mm_n(0)
-            mm_d(0)
-            mm_n(1)
-            mm_d(1)
-            interleave_x('V', 1, 0, 0, 1024)
-            interleave_x('S', 1, 1, 0, 768)
-            interleave_x('V', 1, 1, 768, 1024)
-            pcopy(0)
-            pcopy(1)
-            mm_p(2)
-            mm_p(3)
-            quant_x(1, 0)
-            num_(0)
-            den_(0)
-            empty_g('S', 2, 0)
-            empty_g('S', 2, 1)
-            quant_x(1, 1)
-            pcopy(2)
-            pcopy(3)
-            mm_p(4)
-            mm_p(5)
-            num_(1)
-            den_(1)
-            mm_n(2)
-            mm_d(2)
-            mm_n(3)
-            mm_d(3)
-            quant_g(1)
-            pcopy(4)
-            rsqrt(0, 2)
-            num_(2)
-            den_(2)
-            times_g('G', den, 0, 1)
-            num_(3)
-            den_(3)
-            times_g('G', den, 1, 1)
-            pcopy(5)
-            mm_n(4)
-            mm_d(4)
-            mm_p(6)
-            mm_n(5)
-            mm_d(5)
-            mm_p(7)
-            rsqrt(2, 2)
-            num_(4)
-            den_(4)
-            times_g('G', den, 2, 1)
-            pcopy(6)
-            mm_n(6)
-            mm_d(6)
-            num_(5)
-            den_(5)
-            times_g('G', den, 3, 1)
-            pcopy(7)
-            mm_n(7)
-            mm_d(7)
-            rsqrt(4, 2)
-            num_(6)
-            den_(6)
-            times_g('G', den, 4, 1)
-            mm_p(8)
-            pcopy(8)
-            num_(7)
-            den_(7)
-            times_g('G', den, 5, 1)
-            mm_n(8)
-            mm_d(8)
-            mm_p(9)
-            pcopy(9)
-            rsqrt(6, 2)
-            mm_n(9)
-            mm_d(9)
-            mm_p(10)
-            pcopy(10)
-            times_g('G', den, 6, 1)
-            num_(8)
-            den_(8)
-            times_g('G', den, 7, 1)
-            mm_n(10)
-            mm_d(10)
-            mm_p(11)
-            pcopy(11)
-            num_(9)
-            den_(9)
-            mm_n(11)
-            mm_d(11)
-            rsqrt(8, 2)
-            num_(10)
-            den_(10)
-            sqrt(0, 2)
-            num_(11)
-            den_(11)
-            times_g('V', den, 8, 2)
-            final(0, 2)
-            sqrt(2, 2)
-            final(2, 2)
-            sqrt(10, 2)
-            sqrt(4, 2)
-            times_g('V', num, 10, 2)
-            final(4, 2)
-            sqrt(6, 2)
-            final(6, 2)
-            sqrt(8, 2)
-            final(8, 2)
-            rsqrt(10, 1)
-            final(10, 1)
-            rsqrt(11, 1)
-            final(11, 1)
+        with tc.manual_schedule():
+            nc.scalar.dma_start(out=m_sb[:], in_=m.rearrange("(k q t) -> q k t", q=P, t=PACK))
+            nc.scalar.dma_start(out=x_scale_sb[:], in_=x_scale.rearrange("(k q t) o -> q k (t o)", q=P, t=PACK))
+            nc.gpsimd.dma_start(out=c_row[:], in_=c.partition_broadcast(P))
+            nc.gpsimd.dma_start(out=c_col[:], in_=c.rearrange("(q t) -> q t", t=PACK))
+            nc.gpsimd.dma_start(out=d_col[:], in_=d.rearrange("(q t) -> q t", t=PACK))
+            for lo in range(0, R, R // 2):
+                cols = slice(lo, lo + R // 2)
+                nc.sync.dma_start(out=f_rows[0][:, :, cols], in_=f_view[0, :, :, cols])
+            nc.sync.dma_start(out=f_rows[1][:], in_=f_view[1])
+            for half in range(2):
+                nc.sync.dma_start(out=x_raw[0, half][:], in_=x_view[0, :, 2 * half : 2 * half + 2, :])
+            nc.sync.dma_start(out=g_sb[0][:], in_=g_view[0])
+            for half in range(2):
+                nc.sync.dma_start(out=x_raw[1, half][:], in_=x_view[1, :, 2 * half : 2 * half + 2, :])
+            for h in range(1, LOADS):
+                nc.sync.dma_start(out=g_sb[h][:], in_=g_view[h])
+
+            nc.vector.memset(table_in[:], 1.0)
+            nc.scalar.activation(out=table_out[:], in_=table_in[:], func=ACT.Sqrt)
+            make_identity(nc, ident[:])
+            nc.gpsimd.tensor_tensor(out=e_plus[:], in0=c_col[:], in1=d_col[:], op=ALU.mult)
+            nc.gpsimd.tensor_scalar(out=e_minus[:], in0=e_plus[:], scalar1=-1.0, scalar2=None, op0=ALU.mult)
+
+            for lo in range(0, R, R // 2):
+                interleave_f(vector_copy, 0, lo, lo + R // 2)
+            interleave_f(scalar_copy, 1, 0, F_SCALAR)
+            interleave_f(vector_copy, 1, F_SCALAR, R)
+            for k in range(PASSES):
+                weight_f(k)
+            quantize(
+                f_codes[:].rearrange("p k r -> p (k r)"),
+                f_scales[:].rearrange("p k r -> p (k r)"),
+                f_inter[:].rearrange("p k t q j -> p (k t q j)"),
+            )
+            quantize(
+                fm_codes[:].rearrange("p k r -> p (k r)"),
+                fm_scales[:].rearrange("p k r -> p (k r)"),
+                fm_inter[:].rearrange("p k r j -> p (k r j)"),
+            )
+
+            for k in range(PASSES):
+                for t in range(PACK):
+                    scale_x(0, k, t)
+            for n, tag in enumerate(("p", "gn", "gp", "p")):
+                multiply_a(n, tag)
+            gain_g(0)
+            interleave_x(vector_copy, 0, 0, 0, CHUNKS[0][1])
+            for pair in range(2):
+                turn_g(0, pair)
+            for n in range(R // P):
+                split_a(n)
+            for pair in range(2):
+                scale_x(1, 0, pair)
+                store_turned_g(0, pair)
+            for t in range(2, PACK):
+                scale_x(1, 0, t)
+
+            gain_g(1)
+            for pair in range(2):
+                turn_g(1, pair)
+            interleave_x(vector_copy, 0, 1, 0, CHUNKS[0][1])
+            quantize_x(0, 0)
+            quantize(
+                a_codes[:].rearrange("p z r -> p (z r)"),
+                a_scales[:].rearrange("p z r -> p (z r)"),
+                a_inter[:].rearrange("p z r t -> p (z r t)"),
+            )
+            quantize_gc(0)
+            quantize_x(0, 1)
+            gain_g(2)
+            scale_x(1, 1, 0)
+            for pair in range(2):
+                store_turned_g(1, pair)
+            for pair in range(2):
+                turn_g(2, pair)
+            for t in range(1, PACK):
+                scale_x(1, 1, t)
+
+            for i in range(2):
+                multiply_p(i)
+            for i in range(2):
+                multiply_gn(i)
+                multiply_gp(i)
+            interleave_x(vector_copy, 1, 0, 0, CHUNKS[1][1])
+            interleave_x(scalar_copy, 1, 1, 0, X_SCALAR)
+            interleave_x(vector_copy, 1, 1, X_SCALAR, CHUNKS[1][1])
+            for i in range(2):
+                copy_p(i)
+            for i in range(2, 4):
+                multiply_p(i)
+            quantize_x(1, 0)
+            numerator(0)
+            denominator(0)
+            for pair in range(2):
+                store_turned_g(2, pair)
+            for i in range(2, 4):
+                copy_p(i)
+            quantize_x(1, 1)
+            multiply_gn(2)
+            multiply_gp(2)
+            for i in range(4, 6):
+                multiply_p(i)
+            numerator(1)
+            denominator(1)
+            multiply_gn(3)
+            multiply_gp(3)
+            quantize_gc(1)
+            copy_p(4)
+
+            for i in range(2, 8):
+                if i % 2 == 0:
+                    root_num(i - 2)
+                    for tile in (i - 2, i - 1):
+                        times_g(nc.gpsimd.tensor_tensor, tile, 1)
+                numerator(i)
+                denominator(i)
+                copy_p(i + 3)
+                if i == 2:
+                    multiply_p(6)
+                    multiply_p(7)
+                elif i > 3:
+                    multiply_p(i + 4)
+                multiply_gn(i + 2)
+                multiply_gp(i + 2)
+
+            root_num(6)
+            for tile in (6, 7):
+                times_g(nc.gpsimd.tensor_tensor, tile, 1)
+            for i in (10, 11):
+                multiply_gn(i, tag="turn")
+            numerator(8)
+            numerator(9)
+            copy_p(11)
+            root_num(8)
+            numerator(10)
+            numerator(11)
+            root_num(10)
+            denominator(8)
+            denominator(9)
+            for i in (10, 11):
+                multiply_gp(i)
+            root_den(0, 2)
+            for tile in (8, 9):
+                times_g(nc.gpsimd.tensor_tensor, tile, 1)
+            denominator(10)
+            denominator(11)
+            times_g(nc.vector.tensor_tensor, 10, 2)
+
+            finish(0, 2)
+            for i in range(2, 10, 2):
+                root_den(i, 2)
+                finish(i, 2)
+            root_den(10, 1)
+            finish(10, 1)
+            for lo in range(0, R, R // 2):
+                root_den(11, 1, lo, lo + R // 2)
+            for lo in range(0, R, R // 2):
+                finish(11, 1, lo, lo + R // 2)

from contextlib import ExitStack

import concourse.mybir as mybir
from concourse.masks import make_identity

SAMPLES, N, R = 1024, 1536, 512

F32 = mybir.dt.float32
BF16 = mybir.dt.bfloat16
U32 = mybir.dt.uint32
U8 = mybir.dt.uint8
FP8 = mybir.dt.float8_e4m3fn
FP8X4 = mybir.dt.float8_e4m3fn_x4
ALU = mybir.AluOpType
ACT = mybir.ActivationFunctionType

P = 128
PACK = 4
PASSES = SAMPLES // (P * PACK)
TILES = N // P
LOAD_TILES = 4
LOADS = TILES // LOAD_TILES
CHUNKS = ((0, 512), (512, 1024))
F_SCALAR = 320
X_SCALAR = 768

FLOPS = 2 * N * R * SAMPLES + 2 * R * R * SAMPLES + 2 * 2 * N * R * R


def tile_seminmfsquarerootupdate_kernel(tc, x_bytes, x_scale, f, g, m, c, d, out):
    nc = tc.nc
    with ExitStack() as ctx:
        keep = ctx.enter_context(tc.tile_pool(name="keep", bufs=1))
        work = ctx.enter_context(tc.tile_pool(name="work", bufs=2))
        psum = ctx.enter_context(tc.psum_pool(name="psum", bufs=2))

        ident = keep.tile([P, P], F32, name="ident")
        table_in = keep.tile([P, 1], F32, name="table_in")
        table_out = keep.tile([P, 1], F32, name="table_out")
        m_sb = keep.tile([P, PASSES, PACK], BF16, name="m_sb")
        x_scale_sb = keep.tile([P, PASSES, PACK], F32, name="x_scale_sb")
        c_row = keep.tile([P, R], BF16, name="c_row")
        c_col = keep.tile([P, PACK], BF16, name="c_col")
        d_col = keep.tile([P, PACK], BF16, name="d_col")
        e_minus = keep.tile([P, PACK], F32, name="e_minus")
        e_plus = keep.tile([P, PACK], F32, name="e_plus")

        f_rows = [keep.tile([P, PACK, R], BF16, name="f_rows%d" % k, align_bytes=64) for k in range(PASSES)]
        f_inter = keep.tile([P, PASSES, PACK, P, PACK], BF16, name="f_inter", align_bytes=64)
        fm_inter = keep.tile([P, PASSES, R, PACK], BF16, name="fm_inter", align_bytes=64)
        f_codes = keep.tile([P, PASSES, R], U32, name="f_codes", align_bytes=64)
        f_scales = keep.tile([P, PASSES, R], U8, name="f_scales", align_bytes=64)
        fm_codes = keep.tile([P, PASSES, R], U32, name="fm_codes", align_bytes=64)
        fm_scales = keep.tile([P, PASSES, R], U8, name="fm_scales", align_bytes=64)

        x_raw = {}
        for k in range(PASSES):
            for half in range(2):
                x_raw[k, half] = keep.tile([P, 2, N], U8, name="x_raw%d%d" % (k, half), align_bytes=64)
        x_rows = {}
        x_inter = {}
        x_codes = {}
        x_scales = {}
        gc_inter = []
        gc_codes = []
        gc_scales = []
        for ch, (first, width) in enumerate(CHUNKS):
            for k in range(PASSES):
                x_rows[ch, k] = keep.tile([P, PACK, width], BF16, name="x_rows%d%d" % (ch, k), align_bytes=64)
                x_inter[ch, k] = keep.tile([P, width, PACK], BF16, name="x_inter%d%d" % (ch, k), align_bytes=64)
                x_codes[ch, k] = keep.tile([P, width], U32, name="x_codes%d%d" % (ch, k), align_bytes=64)
                x_scales[ch, k] = keep.tile([P, width], U8, name="x_scales%d%d" % (ch, k), align_bytes=64)
            gc_codes.append(keep.tile([P, width], U32, name="gc_codes%d" % ch, align_bytes=64))
            gc_scales.append(keep.tile([P, width], U8, name="gc_scales%d" % ch, align_bytes=64))
            gc_inter.append(keep.tile([P, width, PACK], BF16, name="gc_inter%d" % ch, align_bytes=64))
        g_sb = [keep.tile([P, LOAD_TILES, R], BF16, name="g_sb%d" % h, align_bytes=64) for h in range(LOADS)]
        a_inter = keep.tile([P, 2, R, PACK], BF16, name="a_inter", align_bytes=64)
        a_codes = keep.tile([P, 2, R], U32, name="a_codes", align_bytes=64)
        a_scales = keep.tile([P, 2, R], U8, name="a_scales", align_bytes=64)
        num = keep.tile([P, TILES, R], F32, name="num")
        den = keep.tile([P, TILES, R], F32, name="den")

        f_view = f.rearrange("(k q t) r -> k q t r", q=P, t=PACK)
        x_view = x_bytes.rearrange("(k q t) n -> k q t n", q=P, t=PACK)
        g_view = g.rearrange("(h i q) r -> h q i r", i=LOAD_TILES, q=P)

        def vector_copy(dst, src):
            nc.vector.tensor_copy(out=dst, in_=src)

        def scalar_copy(dst, src):
            nc.scalar.copy(out=dst, in_=src)

        def quantize(codes, scales, values):
            nc.vector.quantize_mx(out=codes.bitcast(FP8X4), scales=scales, in_=values)

        def interleave_f(copy, k, lo, hi):
            copy(
                f_inter[:, k, :, lo // PACK : hi // PACK, :],
                f_rows[k][:, :, lo:hi].rearrange("p j (q t) -> p t q j", t=PACK),
            )

        def weight_f(k):
            nc.vector.tensor_tensor(
                out=fm_inter[:, k, :, :].rearrange("p (q t) j -> p q t j", t=PACK),
                in0=f_inter[:, k, :, :, :].rearrange("p t q j -> p q t j"),
                in1=m_sb[:, k, :].unsqueeze(1).unsqueeze(1).to_broadcast([P, P, PACK, PACK]),
                op=ALU.mult,
            )

        def scale_x(ch, k, t):
            first, width = CHUNKS[ch]
            nc.scalar.activation(
                out=x_rows[ch, k][:, t, :],
                in_=x_raw[k, t // 2][:, t % 2, first : first + width].bitcast(FP8),
                func=ACT.Copy,
                scale=x_scale_sb[:, k, t : t + 1],
            )

        def interleave_x(copy, ch, k, lo, hi):
            copy(
                x_inter[ch, k][:, lo:hi, :].rearrange("p (n i) t -> p n t i", i=4),
                x_rows[ch, k][:, :, lo:hi].rearrange("p t (n i) -> p n t i", i=4),
            )

        def quantize_x(ch, k):
            quantize(x_codes[ch, k][:], x_scales[ch, k][:], x_inter[ch, k][:].rearrange("p n t -> p (n t)"))

        gc_rows = {}
        gc_turned = {}

        def gain_g(h):
            gc_rows[h] = work.tile([P, LOAD_TILES, R], BF16, name="gc_rows", align_bytes=64)
            nc.vector.tensor_tensor(
                out=gc_rows[h][:],
                in0=g_sb[h][:],
                in1=c_row[:].unsqueeze(1).to_broadcast([P, LOAD_TILES, R]),
                op=ALU.mult,
            )

        def turn_g(h, pair):
            bank = psum.tile([P, 2, 2, P], F32, name="turn", tag="turn", bufs=2)
            for i in range(2):
                words = gc_rows[h][:, 2 * pair + i, :].bitcast(F32)
                for u in range(2):
                    nc.tensor.transpose(bank[:, i, u, :], words[:, u : R // 2 : 2], ident[:])
            gc_turned[h, pair] = bank

        def store_turned_g(h, pair):
            ch = 0 if h == 0 else 1
            words = gc_inter[ch][:].rearrange("p r t -> p (r t)").bitcast(F32)
            start = 2 * ((2 * h + pair) * 2 * P - CHUNKS[ch][0])
            scalar_copy(
                words[:, start : start + 4 * P].rearrange("p (i r u) -> p i r u", i=2, u=2),
                gc_turned[h, pair][:].rearrange("p i u r -> p i r u"),
            )

        def quantize_gc(ch):
            quantize(gc_codes[ch][:], gc_scales[ch][:], gc_inter[ch][:].rearrange("p r t -> p (r t)"))

        a_banks = {}

        def multiply_a(n, tag):
            bank = psum.tile([P, PACK, P], F32, name="a_bank%d" % n, tag=tag, bufs=2)
            for t in range(PACK):
                for k in range(PASSES):
                    nc.tensor.matmul_mx(
                        out=bank[:, t, :],
                        lhsT=f_codes[:, k, t * P : (t + 1) * P].bitcast(FP8X4),
                        lhsT_scale=f_scales[:, k, t * P : (t + 1) * P],
                        rhs=fm_codes[:, k, n * P : (n + 1) * P].bitcast(FP8X4),
                        rhs_scale=fm_scales[:, k, n * P : (n + 1) * P],
                        start=(k == 0),
                        stop=(k == PASSES - 1),
                    )
            a_banks[n] = bank

        def split_a(n):
            for part, (op, e) in enumerate(((ALU.min, e_minus), (ALU.max, e_plus))):
                nc.vector.scalar_tensor_tensor(
                    out=a_inter[:, part, n * P : (n + 1) * P, :],
                    in0=a_banks[n][:].rearrange("p t n -> p n t"),
                    scalar=0.0,
                    in1=e[:].unsqueeze(1).to_broadcast([P, P, PACK]),
                    op0=op,
                    op1=ALU.mult,
                )

        p_banks = {}
        p_sb = {}
        gn_banks = {}
        gp_banks = {}

        def place(i):
            ch = 0 if i * P < CHUNKS[0][1] else 1
            return ch, i * P - CHUNKS[ch][0]

        def multiply_p(i):
            p_banks[i] = psum.tile([P, R], F32, name="p_bank", tag="p", bufs=2)
            ch, o = place(i)
            for k in range(PASSES):
                nc.tensor.matmul_mx(
                    out=p_banks[i][:],
                    lhsT=x_codes[ch, k][:, o : o + P].bitcast(FP8X4),
                    lhsT_scale=x_scales[ch, k][:, o : o + P],
                    rhs=fm_codes[:, k, :].bitcast(FP8X4),
                    rhs_scale=fm_scales[:, k, :],
                    start=(k == 0),
                    stop=(k == PASSES - 1),
                )

        def multiply_gc(bank, i, part):
            ch, o = place(i)
            nc.tensor.matmul_mx(
                out=bank[:],
                lhsT=gc_codes[ch][:, o : o + P].bitcast(FP8X4),
                lhsT_scale=gc_scales[ch][:, o : o + P],
                rhs=a_codes[:, part, :].bitcast(FP8X4),
                rhs_scale=a_scales[:, part, :],
                start=True,
                stop=True,
            )

        def multiply_gn(i, tag="gn"):
            gn_banks[i] = psum.tile([P, R], F32, name="gn_bank", tag=tag, bufs=2)
            multiply_gc(gn_banks[i], i, 0)

        def multiply_gp(i):
            gp_banks[i] = psum.tile([P, R], F32, name="gp_bank", tag="gp", bufs=2)
            multiply_gc(gp_banks[i], i, 1)

        def copy_p(i):
            p_sb[i] = work.tile([P, R], F32, name="p_sb", bufs=8)
            scalar_copy(p_sb[i][:], p_banks[i][:])

        def numerator(i):
            nc.vector.scalar_tensor_tensor(
                out=num[:, i, :], in0=p_sb[i][:], scalar=0.0, in1=gn_banks[i][:], op0=ALU.max, op1=ALU.add
            )

        def denominator(i):
            nc.vector.scalar_tensor_tensor(
                out=den[:, i, :], in0=p_sb[i][:], scalar=0.0, in1=gp_banks[i][:], op0=ALU.min, op1=ALU.subtract
            )

        def root_num(i):
            nc.scalar.activation(out=num[:, i : i + 2, :], in_=num[:, i : i + 2, :], func=ACT.Sqrt)

        def root_den(i, tiles, lo=0, hi=R):
            window = den[:, i : i + tiles, lo:hi]
            nc.scalar.activation(out=window, in_=window, func=ACT.Abs_reciprocal_sqrt)

        def times_g(multiply, i, tiles):
            o = i % LOAD_TILES
            window = num[:, i : i + tiles, :]
            multiply(out=window, in0=window, in1=g_sb[i // LOAD_TILES][:, o : o + tiles, :], op=ALU.mult)

        def finish(i, tiles, lo=0, hi=R):
            window = num[:, i : i + tiles, lo:hi]
            nc.vector.tensor_tensor(out=window, in0=window, in1=den[:, i : i + tiles, lo:hi], op=ALU.mult)
            for tile in range(i, i + tiles):
                nc.sync.dma_start(out=out[tile * P : (tile + 1) * P, lo:hi], in_=num[:, tile, lo:hi])

        with tc.manual_schedule():
            nc.scalar.dma_start(out=m_sb[:], in_=m.rearrange("(k q t) -> q k t", q=P, t=PACK))
            nc.scalar.dma_start(out=x_scale_sb[:], in_=x_scale.rearrange("(k q t) o -> q k (t o)", q=P, t=PACK))
            nc.gpsimd.dma_start(out=c_row[:], in_=c.partition_broadcast(P))
            nc.gpsimd.dma_start(out=c_col[:], in_=c.rearrange("(q t) -> q t", t=PACK))
            nc.gpsimd.dma_start(out=d_col[:], in_=d.rearrange("(q t) -> q t", t=PACK))
            for lo in range(0, R, R // 2):
                cols = slice(lo, lo + R // 2)
                nc.sync.dma_start(out=f_rows[0][:, :, cols], in_=f_view[0, :, :, cols])
            nc.sync.dma_start(out=f_rows[1][:], in_=f_view[1])
            for half in range(2):
                nc.sync.dma_start(out=x_raw[0, half][:], in_=x_view[0, :, 2 * half : 2 * half + 2, :])
            nc.sync.dma_start(out=g_sb[0][:], in_=g_view[0])
            for half in range(2):
                nc.sync.dma_start(out=x_raw[1, half][:], in_=x_view[1, :, 2 * half : 2 * half + 2, :])
            for h in range(1, LOADS):
                nc.sync.dma_start(out=g_sb[h][:], in_=g_view[h])

            nc.vector.memset(table_in[:], 1.0)
            nc.scalar.activation(out=table_out[:], in_=table_in[:], func=ACT.Sqrt)
            make_identity(nc, ident[:])
            nc.gpsimd.tensor_tensor(out=e_plus[:], in0=c_col[:], in1=d_col[:], op=ALU.mult)
            nc.gpsimd.tensor_scalar(out=e_minus[:], in0=e_plus[:], scalar1=-1.0, scalar2=None, op0=ALU.mult)

            for lo in range(0, R, R // 2):
                interleave_f(vector_copy, 0, lo, lo + R // 2)
            interleave_f(scalar_copy, 1, 0, F_SCALAR)
            interleave_f(vector_copy, 1, F_SCALAR, R)
            for k in range(PASSES):
                weight_f(k)
            quantize(
                f_codes[:].rearrange("p k r -> p (k r)"),
                f_scales[:].rearrange("p k r -> p (k r)"),
                f_inter[:].rearrange("p k t q j -> p (k t q j)"),
            )
            quantize(
                fm_codes[:].rearrange("p k r -> p (k r)"),
                fm_scales[:].rearrange("p k r -> p (k r)"),
                fm_inter[:].rearrange("p k r j -> p (k r j)"),
            )

            for k in range(PASSES):
                for t in range(PACK):
                    scale_x(0, k, t)
            for n, tag in enumerate(("p", "gn", "gp", "p")):
                multiply_a(n, tag)
            gain_g(0)
            interleave_x(vector_copy, 0, 0, 0, CHUNKS[0][1])
            for pair in range(2):
                turn_g(0, pair)
            for n in range(R // P):
                split_a(n)
            for pair in range(2):
                scale_x(1, 0, pair)
                store_turned_g(0, pair)
            for t in range(2, PACK):
                scale_x(1, 0, t)

            gain_g(1)
            for pair in range(2):
                turn_g(1, pair)
            interleave_x(vector_copy, 0, 1, 0, CHUNKS[0][1])
            quantize_x(0, 0)
            quantize(
                a_codes[:].rearrange("p z r -> p (z r)"),
                a_scales[:].rearrange("p z r -> p (z r)"),
                a_inter[:].rearrange("p z r t -> p (z r t)"),
            )
            quantize_gc(0)
            quantize_x(0, 1)
            gain_g(2)
            scale_x(1, 1, 0)
            for pair in range(2):
                store_turned_g(1, pair)
            for pair in range(2):
                turn_g(2, pair)
            for t in range(1, PACK):
                scale_x(1, 1, t)

            for i in range(2):
                multiply_p(i)
            for i in range(2):
                multiply_gn(i)
                multiply_gp(i)
            interleave_x(vector_copy, 1, 0, 0, CHUNKS[1][1])
            interleave_x(scalar_copy, 1, 1, 0, X_SCALAR)
            interleave_x(vector_copy, 1, 1, X_SCALAR, CHUNKS[1][1])
            for i in range(2):
                copy_p(i)
            for i in range(2, 4):
                multiply_p(i)
            quantize_x(1, 0)
            numerator(0)
            denominator(0)
            for pair in range(2):
                store_turned_g(2, pair)
            for i in range(2, 4):
                copy_p(i)
            quantize_x(1, 1)
            multiply_gn(2)
            multiply_gp(2)
            for i in range(4, 6):
                multiply_p(i)
            numerator(1)
            denominator(1)
            multiply_gn(3)
            multiply_gp(3)
            quantize_gc(1)
            copy_p(4)

            for i in range(2, 8):
                if i % 2 == 0:
                    root_num(i - 2)
                    for tile in (i - 2, i - 1):
                        times_g(nc.gpsimd.tensor_tensor, tile, 1)
                numerator(i)
                denominator(i)
                copy_p(i + 3)
                if i == 2:
                    multiply_p(6)
                    multiply_p(7)
                elif i > 3:
                    multiply_p(i + 4)
                multiply_gn(i + 2)
                multiply_gp(i + 2)

            root_num(6)
            for tile in (6, 7):
                times_g(nc.gpsimd.tensor_tensor, tile, 1)
            for i in (10, 11):
                multiply_gn(i, tag="turn")
            numerator(8)
            numerator(9)
            copy_p(11)
            root_num(8)
            numerator(10)
            numerator(11)
            root_num(10)
            denominator(8)
            denominator(9)
            for i in (10, 11):
                multiply_gp(i)
            root_den(0, 2)
            for tile in (8, 9):
                times_g(nc.gpsimd.tensor_tensor, tile, 1)
            denominator(10)
            denominator(11)
            times_g(nc.vector.tensor_tensor, 10, 2)

            finish(0, 2)
            for i in range(2, 10, 2):
                root_den(i, 2)
                finish(i, 2)
            root_den(10, 1)
            finish(10, 1)
            for lo in range(0, R, R // 2):
                root_den(11, 1, lo, lo + R // 2)
            for lo in range(0, R, R // 2):
                finish(11, 1, lo, lo + R // 2)
